import numpy as np
import ml_dtypes


def mxq(x, axis, fmt="e4m3"):
    dtype, down = {"e4m3": (ml_dtypes.float8_e4m3fn, 7), "e5m2": (ml_dtypes.float8_e5m2, 14)}[fmt]
    v = np.moveaxis(np.asarray(x, np.float32).astype(ml_dtypes.bfloat16).astype(np.float64), axis, -1)
    blocks = v.reshape(v.shape[:-1] + (-1, 32))
    amax = np.abs(blocks).max(-1, keepdims=True)
    byte = np.maximum(np.where(amax > 0, np.frexp(amax)[1] - 1 + 127, 0) - down, 1)
    scale = np.exp2(byte - 127.0)
    codes = (blocks / scale).astype(np.float32).astype(dtype).astype(np.float64)
    return np.moveaxis((codes * scale).reshape(v.shape), -1, axis)


WIDE = False


def mx_kscale(k):
    if not WIDE:
        return np.ones(k)
    levels = np.array([10, -10, 5, -5, 0])
    if k % 512:
        return np.exp2(np.random.permutation(np.resize(levels, k // 32))).repeat(32)
    a = np.empty((k // 512, 16))
    for p in range(k // 512):
        a[p, :8] = np.random.permutation(np.resize(levels, 8))
        for g in range(8):
            far = levels[np.abs(levels - a[p, g]) >= 10]
            a[p, g + 8] = far[np.random.randint(len(far))]
    return np.exp2(a.ravel()).repeat(32)


def f64(x):
    return np.asarray(x).astype(np.float64)


def striped(idx):
    return np.tile(idx.reshape(-1, 16).T, (8, 1)).astype(np.uint16)


def unstriped(offs):
    return offs[:16].T.reshape(-1).astype(np.int64)


def pack_weight(w):
    k, n = w.shape
    w = f64(np.asarray(w, np.float32).astype(ml_dtypes.bfloat16)).reshape(k // 32, 32, n)
    amax = np.abs(w).max(1)
    byte = np.clip(np.where(amax > 0, np.frexp(amax)[1] - 1 + 127 - 7, 1), 1, 254)
    scaled = (w * np.exp2(127.0 - byte)[:, None, :]).reshape(k, n).astype(np.float32)
    words = np.ascontiguousarray(scaled.reshape(k // 512, 128, 4, n).transpose(0, 1, 3, 2)).astype(ml_dtypes.float8_e4m3fn).view(np.uint8)
    return words, np.ascontiguousarray(byte.astype(np.uint8).reshape(k // 512, 16, n))


def unpack_weight(words, scales):
    g, p, n, _ = words.shape
    vals = np.ascontiguousarray(words).view(ml_dtypes.float8_e4m3fn).astype(np.float64) * np.repeat(np.exp2(scales.astype(np.float64) - 127.0), 8, axis=1)[..., None]
    return vals.transpose(0, 1, 3, 2).reshape(g * 512, n)


E2M1 = np.array([0.0, 0.5, 1.0, 1.5, 2.0, 3.0, 4.0, 6.0, -0.0, -0.5, -1.0, -1.5, -2.0, -3.0, -4.0, -6.0])


def pack_fp4(w):
    k, n = w.shape
    w = f64(np.asarray(w, np.float32).astype(ml_dtypes.bfloat16)).reshape(k // 32, 32, n)
    amax = np.abs(w).max(1)
    mant, ex = np.frexp(amax / 6.0)
    byte = np.clip(np.where(amax > 0, np.where(mant > 0.5, ex, ex - 1) + 127, 1), 1, 254)
    scaled = (w * np.exp2(127.0 - byte)[:, None, :]).reshape(k, n).astype(np.float32)
    c = np.ascontiguousarray(scaled.reshape(k // 512, 128, 4, n).transpose(0, 1, 3, 2)).astype(ml_dtypes.float4_e2m1fn).view(np.uint8) & 0xF
    words = (c[..., 0::2] | (c[..., 1::2] << 4)).reshape(k // 512, 128, 2 * n)
    return np.ascontiguousarray(words), np.ascontiguousarray(byte.astype(np.uint8).reshape(k // 512, 16, n))


def unpack_fp4(words, scales):
    g, _, n = scales.shape
    words = np.ascontiguousarray(words).reshape(g, 128, n, 2)
    nib = np.empty((g, 128, n, 4), np.uint8)
    nib[..., 0::2] = words & 0xF
    nib[..., 1::2] = words >> 4
    vals = E2M1[nib] * np.repeat(np.exp2(scales.astype(np.float64) - 127.0), 8, axis=1)[..., None]
    return vals.transpose(0, 1, 3, 2).reshape(g * 512, n)


def gelu(v):
    return 0.5 * v * (1.0 + np.tanh(np.sqrt(2.0 / np.pi) * (v + 0.044715 * v**3)))


K, T, S, V, H, N = 1024, 2048, 1024, 512, 512, 128


def setup_inputs():
    n = np.random.standard_normal
    s = mx_kscale(K)[:, None]
    u = mx_kscale(H)
    packed_xT = pack_weight(n((K, T)) * s)
    packed_w3 = pack_fp4(n((H, N)) / np.sqrt(H) / u[:, None])
    return {
        "x_words": packed_xT[0],
        "x_scales": packed_xT[1],
        "w1": (n((K, H)) / np.sqrt(2 * K) / s * u).astype(np.float32),
        "w2": (n((K, H)) / np.sqrt(2 * K) / s * u).astype(np.float32),
        "w3_words": packed_w3[0],
        "w3_scales": packed_w3[1],
        "offs": striped(np.random.permutation(T)[:S]),
        "cen": striped(np.random.permutation(S)[:V]),
        "pos1": striped(np.random.permutation(S)[:V]),
        "pos2": striped(np.random.permutation(S)[:V]),
        "pos3": striped(np.random.permutation(S)[:V]),
    }


def reference(x_words, x_scales, w1, w2, w3_words, w3_scales, offs, cen, pos1, pos2, pos3):
    xq = unpack_weight(x_words, x_scales)[:, unstriped(offs)]
    y = mxq(f64(w1), 0, "e4m3").T @ xq
    yc = y[:, unstriped(cen)]
    e = mxq(f64(w2), 0, "e4m3").T @ xq
    z = np.maximum(np.maximum(gelu(yc + e[:, unstriped(pos1)]), gelu(yc + e[:, unstriped(pos2)])), gelu(yc + e[:, unstriped(pos3)]))
    return unpack_fp4(w3_words, w3_scales).T @ mxq(z, 0, "e4m3")

@@ -1,0 +1,250 @@
+from contextlib import ExitStack
+
+import concourse.mybir as mybir
+from concourse.masks import make_identity
+
+K, T, S, V, H, N = 1024, 2048, 1024, 512, 512, 128
+FLOPS = 2 * (2 * K * H * S + H * N * V)
+
+F32 = mybir.dt.float32
+BF16 = mybir.dt.bfloat16
+I32 = mybir.dt.int32
+U32 = mybir.dt.uint32
+U16 = mybir.dt.uint16
+U8 = mybir.dt.uint8
+E4M3 = mybir.dt.float8_e4m3fn_x4
+E2M1 = mybir.dt.float4_e2m1fn_x4
+GELU = mybir.ActivationFunctionType.Gelu_apprx_tanh
+MAX = mybir.AluOpType.max
+
+P = 128
+PACK = 4
+PASSES = K // (P * PACK)
+BANK = 512
+TILES = H // P
+EDGES = 3
+LIST = 16
+BLOCKS = V // P
+PIECES = ((0, 2), (2, 3), (3, 4))
+
+
+def tile_picked_edgecv_gelu_p_kernel(
+    tc, x_words, x_scales, w1, w2, w3_words, w3_scales, offs, cen, pos1, pos2, pos3, out
+):
+    nc = tc.nc
+    with ExitStack() as ctx:
+        lists = ctx.enter_context(tc.tile_pool(name="lists", bufs=1))
+        sb = ctx.enter_context(tc.tile_pool(name="sb", bufs=1))
+        psum = ctx.enter_context(tc.psum_pool(name="psum", bufs=1))
+
+        def load_list(src, name):
+            dst = lists.tile(list(src.shape), U16, name=name)
+            nc.sync.dma_start(dst[:], src)
+            return dst
+
+        def load_words(g):
+            dst = sb.tile([P, T], U32, name=f"x_table{g}", align_bytes=64)
+            nc.sync.dma_start(dst[:].bitcast(I32), x_words[g].rearrange("p n t -> p (n t)").bitcast(I32))
+            return dst
+
+        weights = {"e": w2, "y": w1}
+        raw = {}
+
+        def load_weight(name, t, g):
+            raw[name, t, g] = sb.tile([P, PACK, P], F32, name=f"raw_{name}{t}{g}", align_bytes=64)
+            rows = weights[name][g * P * PACK : (g + 1) * P * PACK, t * P : (t + 1) * P]
+            nc.sync.dma_start(raw[name, t, g][:], rows.rearrange("(p j) c -> p j c", j=PACK))
+
+        scale_table = sb.tile([P, T], U8, name="scale_table", align_bytes=64)
+        nc.vector.memset(scale_table[:].bitcast(I32), 0)
+        w3_scale = sb.tile([P, N], U8, name="w3_scale", align_bytes=64)
+        nc.vector.memset(w3_scale[:].bitcast(I32), 0)
+
+        offs_t = load_list(offs, "offs")
+        pos_t = [load_list(pos1, "pos1")]
+        for q in range(4):
+            nc.sync.dma_start(
+                scale_table[32 * q : 32 * q + 4 * PASSES, :].bitcast(I32), x_scales[:, 4 * q : 4 * q + 4, :].bitcast(I32)
+            )
+        x_table = [load_words(0)]
+        load_weight("e", 0, 0)
+        x_table.append(load_words(1))
+        load_weight("e", 0, 1)
+        load_weight("y", 0, 0)
+        load_weight("y", 0, 1)
+        pos_t.append(load_list(pos2, "pos2"))
+        pos_t.append(load_list(pos3, "pos3"))
+        cen_t = load_list(cen, "cen")
+        for t in range(1, TILES):
+            for name in weights:
+                for g in range(PASSES):
+                    load_weight(name, t, g)
+        w3_code = sb.tile([P, 2 * N], U8, name="w3_code", align_bytes=64)
+        nc.sync.dma_start(w3_code[:].bitcast(I32), w3_words[0].bitcast(I32))
+        for q in range(4):
+            nc.sync.dma_start(w3_scale[32 * q : 32 * q + 4, :].bitcast(I32), w3_scales[0, 4 * q : 4 * q + 4, :].bitcast(I32))
+
+        identity = sb.tile([P, P], F32, name="identity")
+        make_identity(nc, identity[:])
+        warm = sb.tile([P, 1], F32, name="warm")
+        nc.scalar.activation(warm[:], identity[:, 0:1], GELU)
+
+        x_scale = sb.tile([P, S], U8, name="x_scale", align_bytes=64)
+        x_code = [sb.tile([P, S], U32, name=f"x_code{g}", align_bytes=64) for g in range(PASSES)]
+
+        def pick_words(g, lo, hi):
+            nc.vector.tensor_copy(x_code[g][:, lo:hi], x_table[g][:].indirect(offs_t[:, lo // LIST : hi // LIST]))
+
+        w_code, w_scale, w_bf = {}, {}, {}
+
+        def round_weight(name, t, g):
+            if g == 0:
+                w_bf[name, t] = sb.tile([P, PASSES, P, PACK], BF16, name=f"w_bf_{name}{t}", align_bytes=64)
+                w_code[name, t] = sb.tile([P, PASSES, P], U32, name=f"w_code_{name}{t}", align_bytes=64)
+                w_scale[name, t] = sb.tile([P, PASSES, P], U8, name=f"w_scale_{name}{t}", align_bytes=64)
+            copy = nc.vector.tensor_copy if (name, t) == ("y", 0) else nc.scalar.copy
+            copy(
+                w_bf[name, t][:, g].rearrange("p (c i) j -> p c j i", i=4),
+                raw[name, t, g][:].rearrange("p j (c i) -> p c j i", i=4),
+            )
+
+        def quantize_weight(name, t, lo, hi):
+            nc.vector.quantize_mx(
+                out=w_code[name, t][:, lo:hi].rearrange("p g c -> p (g c)").bitcast(E4M3),
+                scales=w_scale[name, t][:, lo:hi].rearrange("p g c -> p (g c)"),
+                in_=w_bf[name, t][:, lo:hi].rearrange("p g c j -> p (g c j)"),
+            )
+
+        def prepare(name, t):
+            for g in range(PASSES):
+                round_weight(name, t, g)
+            quantize_weight(name, t, 0, PASSES)
+
+        def bank(n):
+            return f"bank{n % 8}"
+
+        rows = {}
+
+        def project(name, t):
+            after = {"e": f"raw_y{t}1", "y": f"raw_e{t + 1}1"}[name]
+            if (name, t) in (("e", 0), ("y", TILES - 1)):
+                after = f"rows_{name}{t}"
+            rows[name, t] = sb.tile([P, S], F32, name=f"rows_{name}{t}", tag=after, align_bytes=64)
+            first = 4 * t + (0 if name == "e" else 2)
+            banks = [psum.tile([P, BANK], F32, name=f"acc_{name}{t}{h}", tag=bank(first + h)) for h in range(S // BANK)]
+            for g in range(PASSES):
+                for h in range(S // BANK):
+                    cols = slice(h * BANK, (h + 1) * BANK)
+                    nc.tensor.matmul_mx(
+                        out=banks[h][:],
+                        lhsT=w_code[name, t][:, g].bitcast(E4M3),
+                        lhsT_scale=w_scale[name, t][:, g],
+                        rhs=x_code[g][:, cols].bitcast(E4M3),
+                        rhs_scale=x_scale[4 * g :, cols],
+                        start=(g == 0),
+                        stop=(g == PASSES - 1),
+                    )
+            for h in range(S // BANK):
+                nc.scalar.copy(rows[name, t][:, h * BANK : (h + 1) * BANK], banks[h][:])
+
+        centre, ends, feats = {}, {}, {}
+
+        def fetch_end(t, d):
+            after = {0: f"w_bf_y{t}", 1: f"end{t}", 2: f"w_bf_e{t + 1}"}[d]
+            ends[t, d] = sb.tile([P, V], F32, name=f"end{t}{d}", tag=after, align_bytes=64)
+            nc.vector.tensor_copy(ends[t, d][:], rows["e", t][:].indirect(pos_t[d][:]))
+
+        def fetch_centre(t, b0, b1):
+            for b in range(b0, b1):
+                centre[t, b] = (b0, b - b0)
+            centre[t, "tile", b0] = sb.tile([P, (b1 - b0) * P], F32, name=f"centre{t}{b0}")
+            nc.vector.tensor_copy(centre[t, "tile", b0][:], rows["y", t][:].indirect(cen_t[:, b0 * P // LIST : b1 * P // LIST]))
+
+        sums = {}
+
+        def turn_ends(t):
+            for b in range(BLOCKS):
+                sums[t, b] = psum.tile([P, EDGES, P], F32, name=f"sums{t}{b}", tag=bank(4 * (t + 1) + b))
+            for d in range(EDGES):
+                for b in range(BLOCKS):
+                    nc.tensor.matmul(
+                        sums[t, b][:, d], ends[t, d][:, b * P : (b + 1) * P], identity[:], start=(d == 0), stop=False, is_transpose=True
+                    )
+
+        def edge_features(t, b0, b1):
+            feats[t, b0] = sb.tile([P, b1 - b0, EDGES, P], BF16, name=f"feat{t}{b0}")
+            for b in range(b0, b1):
+                c0, c = centre[t, b]
+                for d in range(EDGES):
+                    nc.tensor.matmul(
+                        sums[t, b][:, d], centre[t, "tile", c0][:, c * P : (c + 1) * P], identity[:],
+                        start=False, stop=(d == EDGES - 1), is_transpose=True,
+                    )
+                nc.scalar.activation(feats[t, b0][:, b - b0], sums[t, b][:], GELU)
+
+        z_t = {b0: sb.tile([P, b1 - b0, H], BF16, name=f"z_t{b0}") for b0, b1 in PIECES}
+
+        def largest(t, b0, b1):
+            pair = sb.tile([P, b1 - b0, P], BF16, name=f"pair{t}{b0}")
+            nc.vector.tensor_tensor(pair[:], feats[t, b0][:, :, 0], feats[t, b0][:, :, 1], MAX)
+            for c0, c1 in PIECES:
+                if b0 <= c0 and c1 <= b1:
+                    own = slice(c0 - b0, c1 - b0)
+                    nc.vector.tensor_tensor(z_t[c0][:, :, t * P : (t + 1) * P], pair[:, own], feats[t, b0][:, own, 2], MAX)
+
+        def finish(b0, b1):
+            nb = b1 - b0
+            words = z_t[b0][:].bitcast(F32)
+            turned = psum.tile([P, nb, 2, P], F32, name=f"turned{b0}", tag=bank(4 + b0))
+            for b in range(nb):
+                for u in range(2):
+                    nc.tensor.transpose(turned[:, b, u], words[:, b, u::2], identity[:])
+            z_bf = sb.tile([P, nb, P, PACK], BF16, name=f"z_bf{b0}", align_bytes=64)
+            copy = nc.vector.tensor_copy if b0 == 0 else nc.scalar.copy
+            copy(z_bf[:].bitcast(F32), turned[:].rearrange("p b u v -> p b v u"))
+            z_code = sb.tile([P, nb * P], U32, name=f"z_code{b0}", align_bytes=64)
+            z_scale = sb.tile([P, nb * P], U8, name=f"z_scale{b0}", align_bytes=64)
+            nc.vector.quantize_mx(out=z_code[:].bitcast(E4M3), scales=z_scale[:], in_=z_bf[:].rearrange("p b v j -> p (b v j)"))
+            acc = psum.tile([P, nb * P], F32, name=f"out{b0}", tag=bank(b0))
+            nc.tensor.matmul_mx(
+                out=acc[:], lhsT=w3_code[:].bitcast(E2M1), lhsT_scale=w3_scale[:],
+                rhs=z_code[:].bitcast(E4M3), rhs_scale=z_scale[:], start=True, stop=True,
+            )
+            result = sb.tile([P, nb * P], F32, name=f"result{b0}")
+            nc.scalar.copy(result[:], acc[:])
+            nc.sync.dma_start(out[:, b0 * P : b1 * P], result[:])
+
+        nc.vector.tensor_copy(x_scale[:], scale_table[:].indirect(offs_t[:]))
+        pick_words(0, 0, S)
+        round_weight("e", 0, 0)
+        quantize_weight("e", 0, 0, 1)
+        pick_words(1, 0, BANK)
+        round_weight("e", 0, 1)
+        quantize_weight("e", 0, 1, 2)
+        pick_words(1, BANK, S)
+        project("e", 0)
+        prepare("y", 0)
+
+        last = TILES - 1
+        for t in range(TILES):
+            fetch_end(t, 0)
+            fetch_end(t, 1)
+            if t < last:
+                prepare("e", t + 1)
+            project("y", t)
+            fetch_end(t, 2)
+            if t < last:
+                prepare("y", t + 1)
+                fetch_centre(t, 0, BLOCKS)
+                project("e", t + 1)
+            if t > 0:
+                turn_ends(t - 1)
+                edge_features(t - 1, 0, BLOCKS)
+                largest(t - 1, 0, BLOCKS)
+        turn_ends(last)
+        for b0, b1 in PIECES:
+            fetch_centre(last, b0, b1)
+            edge_features(last, b0, b1)
+        for b0, b1 in PIECES:
+            largest(last, b0, b1)
+            finish(b0, b1)

@@ -25,7 +25,17 @@ TILES = H // P
 EDGES = 3
 LIST = 16
 BLOCKS = V // P
-PIECES = ((0, 2), (2, 3), (3, 4))
+ACC_BANKS = (0, 2, 0, 5, 0, 0, 0, 0)
+CENTRE = EDGES
+VEV = 1
+GP = ((0, 2), (2, 4))
+ZV = ()
+OV = ()
+CFIRST = 0
+SLOTS = (1, 3, 5, 7, 9, 11)
+HOLD = 0
+GELU_AT = {0: 12, 1: 13, 2: 15}
+PIECES = ((0, 1), (1, 2), (2, 3), (3, 4))
 
 
 def tile_picked_edgecv_gelu_p_kernel(
@@ -49,6 +59,7 @@ def tile_picked_edgecv_gelu_p_kernel(
 
         weights = {"e": w2, "y": w1}
         raw = {}
+        order = [(name, t) for t in range(TILES) for name in ("ye" if t == TILES - 1 else "ey")]
 
         def load_weight(name, t, g):
             raw[name, t, g] = sb.tile([P, PACK, P], F32, name=f"raw_{name}{t}{g}", align_bytes=64)
@@ -58,7 +69,7 @@ def tile_picked_edgecv_gelu_p_kernel(
         scale_table = sb.tile([P, T], U8, name="scale_table", align_bytes=64)
         nc.vector.memset(scale_table[:].bitcast(I32), 0)
         w3_scale = sb.tile([P, N], U8, name="w3_scale", align_bytes=64)
-        nc.vector.memset(w3_scale[:].bitcast(I32), 0)
+        nc.gpsimd.memset(w3_scale[:].bitcast(I32), 0)
 
         offs_t = load_list(offs, "offs")
         pos_t = [load_list(pos1, "pos1")]
@@ -66,19 +77,17 @@ def tile_picked_edgecv_gelu_p_kernel(
             nc.sync.dma_start(
                 scale_table[32 * q : 32 * q + 4 * PASSES, :].bitcast(I32), x_scales[:, 4 * q : 4 * q + 4, :].bitcast(I32)
             )
-        x_table = [load_words(0)]
+        x_table = [load_words(g) for g in range(PASSES)]
         load_weight("e", 0, 0)
-        x_table.append(load_words(1))
         load_weight("e", 0, 1)
         load_weight("y", 0, 0)
         load_weight("y", 0, 1)
         pos_t.append(load_list(pos2, "pos2"))
         pos_t.append(load_list(pos3, "pos3"))
         cen_t = load_list(cen, "cen")
-        for t in range(1, TILES):
-            for name in weights:
-                for g in range(PASSES):
-                    load_weight(name, t, g)
+        for name, t in order[2:]:
+            for g in range(PASSES):
+                load_weight(name, t, g)
         w3_code = sb.tile([P, 2 * N], U8, name="w3_code", align_bytes=64)
         nc.sync.dma_start(w3_code[:].bitcast(I32), w3_words[0].bitcast(I32))
         for q in range(4):
@@ -90,22 +99,28 @@ def tile_picked_edgecv_gelu_p_kernel(
         nc.scalar.activation(warm[:], identity[:, 0:1], GELU)
 
         x_scale = sb.tile([P, S], U8, name="x_scale", align_bytes=64)
-        x_code = [sb.tile([P, S], U32, name=f"x_code{g}", align_bytes=64) for g in range(PASSES)]
+        x_code = {}
 
-        def pick_words(g, lo, hi):
-            nc.vector.tensor_copy(x_code[g][:, lo:hi], x_table[g][:].indirect(offs_t[:, lo // LIST : hi // LIST]))
+        def pick_words(g, lo, hi, after=None):
+            name = f"x_code{g}{lo}"
+            dst = sb.tile([P, hi - lo], U32, name=name, tag=after or name, align_bytes=64)
+            nc.vector.tensor_copy(dst[:], x_table[g][:].indirect(offs_t[:, lo // LIST : hi // LIST]))
+            for h in range(lo // BANK, hi // BANK):
+                x_code[g, h] = dst[:, h * BANK - lo : (h + 1) * BANK - lo]
 
         w_code, w_scale, w_bf = {}, {}, {}
 
+        def bf_tag(k):
+            return f"w_code_{order[k - 2][0]}{order[k - 2][1]}" if k >= 2 else f"w_bf{k}"
+
         def round_weight(name, t, g):
             if g == 0:
-                w_bf[name, t] = sb.tile([P, PASSES, P, PACK], BF16, name=f"w_bf_{name}{t}", align_bytes=64)
+                w_bf[name, t] = sb.tile([P, PASSES, P, PACK], BF16, name=f"w_bf_{name}{t}", tag=bf_tag(order.index((name, t))), align_bytes=64)
                 w_code[name, t] = sb.tile([P, PASSES, P], U32, name=f"w_code_{name}{t}", align_bytes=64)
                 w_scale[name, t] = sb.tile([P, PASSES, P], U8, name=f"w_scale_{name}{t}", align_bytes=64)
-            copy = nc.vector.tensor_copy if (name, t) == ("y", 0) else nc.scalar.copy
-            copy(
-                w_bf[name, t][:, g].rearrange("p (c i) j -> p c j i", i=4),
-                raw[name, t, g][:].rearrange("p j (c i) -> p c j i", i=4),
+            nc.scalar.copy(
+                w_bf[name, t][:, g].rearrange("p (u m e) j -> p m j u e", u=2, e=2),
+                raw[name, t, g][:].rearrange("p j (m u e) -> p m j u e", u=2, e=2),
             )
 
         def quantize_weight(name, t, lo, hi):
@@ -126,125 +141,132 @@ def tile_picked_edgecv_gelu_p_kernel(
         rows = {}
 
         def project(name, t):
-            after = {"e": f"raw_y{t}1", "y": f"raw_e{t + 1}1"}[name]
-            if (name, t) in (("e", 0), ("y", TILES - 1)):
-                after = f"rows_{name}{t}"
+            k = order.index((name, t))
+            after = f"raw_{order[k + 1][0]}{order[k + 1][1]}0" if 0 < k < len(order) - 1 else f"rows_{name}{t}"
             rows[name, t] = sb.tile([P, S], F32, name=f"rows_{name}{t}", tag=after, align_bytes=64)
-            first = 4 * t + (0 if name == "e" else 2)
+            first = ACC_BANKS[order.index((name, t))]
             banks = [psum.tile([P, BANK], F32, name=f"acc_{name}{t}{h}", tag=bank(first + h)) for h in range(S // BANK)]
-            for g in range(PASSES):
-                for h in range(S // BANK):
+            for g, h in (((0, 0), (0, 1), (1, 0), (1, 1)) if (name, t) == ("e", 0) else ((0, 0), (1, 0), (0, 1), (1, 1))):
+                if True:
                     cols = slice(h * BANK, (h + 1) * BANK)
                     nc.tensor.matmul_mx(
                         out=banks[h][:],
                         lhsT=w_code[name, t][:, g].bitcast(E4M3),
                         lhsT_scale=w_scale[name, t][:, g],
-                        rhs=x_code[g][:, cols].bitcast(E4M3),
+                        rhs=x_code[g, h].bitcast(E4M3),
                         rhs_scale=x_scale[4 * g :, cols],
                         start=(g == 0),
                         stop=(g == PASSES - 1),
                     )
             for h in range(S // BANK):
-                nc.scalar.copy(rows[name, t][:, h * BANK : (h + 1) * BANK], banks[h][:])
+                copy = nc.vector.tensor_copy if k == 0 and h == 0 and VEV else nc.scalar.copy
+                copy(rows[name, t][:, h * BANK : (h + 1) * BANK], banks[h][:])
 
-        centre, ends, feats = {}, {}, {}
+        last = TILES - 1
+        fetched = {}
 
-        def fetch_end(t, d):
-            after = {0: f"w_bf_y{t}", 1: f"end{t}", 2: f"w_bf_e{t + 1}"}[d]
-            ends[t, d] = sb.tile([P, V], F32, name=f"end{t}{d}", tag=after, align_bytes=64)
-            nc.vector.tensor_copy(ends[t, d][:], rows["e", t][:].indirect(pos_t[d][:]))
-
-        def fetch_centre(t, b0, b1):
+        def fetch(t, d, b0, b1, after):
+            source, index = (rows["e", t], pos_t[d]) if d < EDGES else (rows["y", t], cen_t)
+            name = f"fetched{t}{d}{b0}"
+            dst = sb.tile([P, (b1 - b0) * P], F32, name=name, tag=after or name, align_bytes=64)
+            nc.vector.tensor_copy(dst[:], source[:].indirect(index[:, b0 * P // LIST : b1 * P // LIST]))
             for b in range(b0, b1):
-                centre[t, b] = (b0, b - b0)
-            centre[t, "tile", b0] = sb.tile([P, (b1 - b0) * P], F32, name=f"centre{t}{b0}")
-            nc.vector.tensor_copy(centre[t, "tile", b0][:], rows["y", t][:].indirect(cen_t[:, b0 * P // LIST : b1 * P // LIST]))
+                fetched[t, d, b] = dst[:, (b - b0) * P : (b - b0 + 1) * P]
 
-        sums = {}
-
-        def turn_ends(t):
+        def fetch_last():
+            dst = sb.tile([P, V], F32, name="fetched_last")
+            for b0, b1 in GP:
+                nc.vector.tensor_copy(dst[:, b0 * P : b1 * P], rows["e", last][:].indirect(pos_t[2][:, b0 * P // LIST : b1 * P // LIST]))
             for b in range(BLOCKS):
-                sums[t, b] = psum.tile([P, EDGES, P], F32, name=f"sums{t}{b}", tag=bank(4 * (t + 1) + b))
-            for d in range(EDGES):
-                for b in range(BLOCKS):
-                    nc.tensor.matmul(
-                        sums[t, b][:, d], ends[t, d][:, b * P : (b + 1) * P], identity[:], start=(d == 0), stop=False, is_transpose=True
-                    )
+                fetched[last, 2, b] = dst[:, b * P : (b + 1) * P]
 
-        def edge_features(t, b0, b1):
-            feats[t, b0] = sb.tile([P, b1 - b0, EDGES, P], BF16, name=f"feat{t}{b0}")
+        feats = sb.tile([P, TILES, EDGES, V], BF16, name="feats")
+
+        def edge_features(t, d, b0, b1, where):
+            sums = psum.tile([P, b1 - b0, P], F32, name=f"sums{t}{d}{b0}", tag=bank(where))
+            first, second = (CENTRE, d) if d == EDGES - 1 or t == last or CFIRST else (d, CENTRE)
             for b in range(b0, b1):
-                c0, c = centre[t, b]
-                for d in range(EDGES):
-                    nc.tensor.matmul(
-                        sums[t, b][:, d], centre[t, "tile", c0][:, c * P : (c + 1) * P], identity[:],
-                        start=False, stop=(d == EDGES - 1), is_transpose=True,
-                    )
-                nc.scalar.activation(feats[t, b0][:, b - b0], sums[t, b][:], GELU)
+                nc.tensor.matmul(sums[:, b - b0], fetched[t, first, b], identity[:], start=(b == b0), stop=False, is_transpose=True)
+            for b in range(b0, b1):
+                nc.tensor.matmul(sums[:, b - b0], fetched[t, second, b], identity[:], start=False, stop=(b == b1 - 1), is_transpose=True)
+            nc.scalar.activation(feats[:, t, d, b0 * P : b1 * P], sums[:].rearrange("p b i -> p (b i)"), GELU)
 
-        z_t = {b0: sb.tile([P, b1 - b0, H], BF16, name=f"z_t{b0}") for b0, b1 in PIECES}
+        z_row = sb.tile([P, BLOCKS * H], BF16, name="z_row")
+        z_t = z_row[:].rearrange("p (r t c) -> p t r c", t=TILES, c=P // 2)
+        pair = sb.tile([P, TILES, V], BF16, name="pair")
 
-        def largest(t, b0, b1):
-            pair = sb.tile([P, b1 - b0, P], BF16, name=f"pair{t}{b0}")
-            nc.vector.tensor_tensor(pair[:], feats[t, b0][:, :, 0], feats[t, b0][:, :, 1], MAX)
-            for c0, c1 in PIECES:
-                if b0 <= c0 and c1 <= b1:
-                    own = slice(c0 - b0, c1 - b0)
-                    nc.vector.tensor_tensor(z_t[c0][:, :, t * P : (t + 1) * P], pair[:, own], feats[t, b0][:, own, 2], MAX)
+        def larger(t0, t1):
+            nc.vector.tensor_tensor(pair[:, t0:t1], feats[:, t0:t1, 0], feats[:, t0:t1, 1], MAX)
+
+        def largest(t0, t1, b0, b1):
+            cols = slice(b0 * P, b1 * P)
+            nc.vector.tensor_tensor(
+                z_t[:, t0:t1, 2 * b0 : 2 * b1],
+                pair[:, t0:t1, cols].rearrange("p t (r c) -> p t r c", c=P // 2),
+                feats[:, t0:t1, 2, cols].rearrange("p t (r c) -> p t r c", c=P // 2),
+                MAX,
+            )
 
         def finish(b0, b1):
             nb = b1 - b0
-            words = z_t[b0][:].bitcast(F32)
-            turned = psum.tile([P, nb, 2, P], F32, name=f"turned{b0}", tag=bank(4 + b0))
+            words = z_row[:, b0 * H : b1 * H].bitcast(F32)
+            turned = psum.tile([P, nb, 2, P], F32, name=f"turned{b0}", tag=bank((3, 4, 0, 1)[b0]))
             for b in range(nb):
                 for u in range(2):
-                    nc.tensor.transpose(turned[:, b, u], words[:, b, u::2], identity[:])
+                    r = 2 * b + u
+                    nc.tensor.transpose(turned[:, b, u], words[:, r * P : (r + 1) * P], identity[:])
             z_bf = sb.tile([P, nb, P, PACK], BF16, name=f"z_bf{b0}", align_bytes=64)
-            copy = nc.vector.tensor_copy if b0 == 0 else nc.scalar.copy
+            copy = nc.vector.tensor_copy if b0 in ZV else nc.scalar.copy
             copy(z_bf[:].bitcast(F32), turned[:].rearrange("p b u v -> p b v u"))
             z_code = sb.tile([P, nb * P], U32, name=f"z_code{b0}", align_bytes=64)
             z_scale = sb.tile([P, nb * P], U8, name=f"z_scale{b0}", align_bytes=64)
             nc.vector.quantize_mx(out=z_code[:].bitcast(E4M3), scales=z_scale[:], in_=z_bf[:].rearrange("p b v j -> p (b v j)"))
-            acc = psum.tile([P, nb * P], F32, name=f"out{b0}", tag=bank(b0))
+            acc = psum.tile([P, nb * P], F32, name=f"out{b0}", tag=bank((5, 6, 7, 2)[b0]))
             nc.tensor.matmul_mx(
                 out=acc[:], lhsT=w3_code[:].bitcast(E2M1), lhsT_scale=w3_scale[:],
                 rhs=z_code[:].bitcast(E4M3), rhs_scale=z_scale[:], start=True, stop=True,
             )
             result = sb.tile([P, nb * P], F32, name=f"result{b0}")
-            nc.scalar.copy(result[:], acc[:])
+            copy = nc.vector.tensor_copy if b0 in OV else nc.scalar.copy
+            copy(result[:], acc[:])
             nc.sync.dma_start(out[:, b0 * P : b1 * P], result[:])
 
         nc.vector.tensor_copy(x_scale[:], scale_table[:].indirect(offs_t[:]))
         pick_words(0, 0, S)
+        pick_words(1, 0, BANK)
         round_weight("e", 0, 0)
         quantize_weight("e", 0, 0, 1)
-        pick_words(1, 0, BANK)
+        pick_words(1, BANK, S, "raw_e00")
         round_weight("e", 0, 1)
         quantize_weight("e", 0, 1, 2)
-        pick_words(1, BANK, S)
         project("e", 0)
         prepare("y", 0)
 
-        last = TILES - 1
-        for t in range(TILES):
-            fetch_end(t, 0)
-            fetch_end(t, 1)
-            if t < last:
-                prepare("e", t + 1)
-            project("y", t)
-            fetch_end(t, 2)
-            if t < last:
-                prepare("y", t + 1)
-                fetch_centre(t, 0, BLOCKS)
-                project("e", t + 1)
-            if t > 0:
-                turn_ends(t - 1)
-                edge_features(t - 1, 0, BLOCKS)
-                largest(t - 1, 0, BLOCKS)
-        turn_ends(last)
+        for n in range(4 * TILES - 1):
+            t, d = n // 4, ((0, 1, CENTRE, 2) if n // 4 < last else (CENTRE, 0, 1))[n % 4]
+            after = None
+            if n in SLOTS:
+                k = SLOTS.index(n) + 2
+                prepare(*order[k])
+                project(*order[k - 1])
+                after = f"raw_{order[k][0]}{order[k][1]}1"
+            elif HOLD and n - 1 in SLOTS:
+                after = bf_tag(SLOTS.index(n - 1) + 2)
+            if n == SLOTS[-1] + 1:
+                project(*order[-1])
+            fetch(t, d, 0, BLOCKS, after)
+            for s in range(last):
+                if GELU_AT[s] == n + 1:
+                    for e in range(EDGES):
+                        edge_features(s, e, 0, BLOCKS, (2, 5, 2)[s] + e)
+                    if s == last - 1:
+                        larger(0, last)
+        edge_features(last, 0, 0, BLOCKS, 0)
+        edge_features(last, 1, 0, BLOCKS, 1)
+        fetch_last()
+        for n, (b0, b1) in enumerate(GP):
+            edge_features(last, 2, b0, b1, (5, 6, 7, 2)[n])
+        larger(last, TILES)
         for b0, b1 in PIECES:
-            fetch_centre(last, b0, b1)
-            edge_features(last, b0, b1)
-        for b0, b1 in PIECES:
-            largest(last, b0, b1)
+            largest(0, TILES, b0, b1)
             finish(b0, b1)

@@ -27,14 +27,15 @@ LIST = 16
 BLOCKS = V // P
 ACC_BANKS = (0, 2, 0, 5, 0, 0, 0, 0)
 CENTRE = EDGES
-VEV = 1
+VEV = (0,)
+CUTS = ((0, 512), (512, 768), (768, 1024))
 GP = ((0, 2), (2, 4))
 ZV = ()
 OV = ()
 CFIRST = 0
-SLOTS = (1, 3, 5, 7, 9, 11)
-HOLD = 0
-GELU_AT = {0: 12, 1: 13, 2: 15}
+SLOTS = (1, 3, 4, 6, 8, 10)
+HOLD = 1
+GELU_AT = {0: 11, 1: 13, 2: 15}
 PIECES = ((0, 1), (1, 2), (2, 3), (3, 4))
 
 
@@ -72,16 +73,17 @@ def tile_picked_edgecv_gelu_p_kernel(
         nc.gpsimd.memset(w3_scale[:].bitcast(I32), 0)
 
         offs_t = load_list(offs, "offs")
-        pos_t = [load_list(pos1, "pos1")]
+        x_table = [load_words(0)]
         for q in range(4):
             nc.sync.dma_start(
                 scale_table[32 * q : 32 * q + 4 * PASSES, :].bitcast(I32), x_scales[:, 4 * q : 4 * q + 4, :].bitcast(I32)
             )
-        x_table = [load_words(g) for g in range(PASSES)]
         load_weight("e", 0, 0)
+        x_table.append(load_words(1))
         load_weight("e", 0, 1)
         load_weight("y", 0, 0)
         load_weight("y", 0, 1)
+        pos_t = [load_list(pos1, "pos1")]
         pos_t.append(load_list(pos2, "pos2"))
         pos_t.append(load_list(pos3, "pos3"))
         cen_t = load_list(cen, "cen")
@@ -95,18 +97,19 @@ def tile_picked_edgecv_gelu_p_kernel(
 
         identity = sb.tile([P, P], F32, name="identity")
         make_identity(nc, identity[:])
-        warm = sb.tile([P, 1], F32, name="warm")
-        nc.scalar.activation(warm[:], identity[:, 0:1], GELU)
+        zero = sb.tile([P, 1], F32, name="zero")
+        nc.vector.memset(zero[:], 0.0)
+        no_bias = sb.tile([P, 1], F32, name="no_bias")
+        nc.scalar.activation(no_bias[:], zero[:], GELU)
 
         x_scale = sb.tile([P, S], U8, name="x_scale", align_bytes=64)
-        x_code = {}
+        x_code = [[] for g in range(PASSES)]
 
         def pick_words(g, lo, hi, after=None):
             name = f"x_code{g}{lo}"
             dst = sb.tile([P, hi - lo], U32, name=name, tag=after or name, align_bytes=64)
             nc.vector.tensor_copy(dst[:], x_table[g][:].indirect(offs_t[:, lo // LIST : hi // LIST]))
-            for h in range(lo // BANK, hi // BANK):
-                x_code[g, h] = dst[:, h * BANK - lo : (h + 1) * BANK - lo]
+            x_code[g].append((lo, hi, dst))
 
         w_code, w_scale, w_bf = {}, {}, {}
 
@@ -144,23 +147,27 @@ def tile_picked_edgecv_gelu_p_kernel(
             k = order.index((name, t))
             after = f"raw_{order[k + 1][0]}{order[k + 1][1]}0" if 0 < k < len(order) - 1 else f"rows_{name}{t}"
             rows[name, t] = sb.tile([P, S], F32, name=f"rows_{name}{t}", tag=after, align_bytes=64)
-            first = ACC_BANKS[order.index((name, t))]
-            banks = [psum.tile([P, BANK], F32, name=f"acc_{name}{t}{h}", tag=bank(first + h)) for h in range(S // BANK)]
-            for g, h in (((0, 0), (0, 1), (1, 0), (1, 1)) if (name, t) == ("e", 0) else ((0, 0), (1, 0), (0, 1), (1, 1))):
-                if True:
-                    cols = slice(h * BANK, (h + 1) * BANK)
+            spans = CUTS if k == 0 else ((0, BANK), (BANK, S))
+            banks = [psum.tile([P, hi - lo], F32, name=f"acc_{name}{t}{lo}", tag=bank((0, 1, 4)[h] if k == 0 else ACC_BANKS[k] + h)) for h, (lo, hi) in enumerate(spans)]
+            steps = [(g, h) for g in range(PASSES) for h in range(len(spans))]
+            if k > 0:
+                steps.sort(key=lambda s: s[1])
+            for g, h in steps:
+                lo, hi = spans[h]
+                parts = [(max(lo, a), min(hi, b), a, src) for a, b, src in x_code[g] if max(lo, a) < min(hi, b)]
+                for c0, c1, a, src in parts:
                     nc.tensor.matmul_mx(
-                        out=banks[h][:],
+                        out=banks[h][:, c0 - lo : c1 - lo],
                         lhsT=w_code[name, t][:, g].bitcast(E4M3),
                         lhsT_scale=w_scale[name, t][:, g],
-                        rhs=x_code[g, h].bitcast(E4M3),
-                        rhs_scale=x_scale[4 * g :, cols],
+                        rhs=src[:, c0 - a : c1 - a].bitcast(E4M3),
+                        rhs_scale=x_scale[4 * g :, c0:c1],
                         start=(g == 0),
-                        stop=(g == PASSES - 1),
+                        stop=(g == PASSES - 1 and c1 == hi),
                     )
-            for h in range(S // BANK):
-                copy = nc.vector.tensor_copy if k == 0 and h == 0 and VEV else nc.scalar.copy
-                copy(rows[name, t][:, h * BANK : (h + 1) * BANK], banks[h][:])
+            for h, (lo, hi) in enumerate(spans):
+                copy = nc.vector.tensor_copy if k == 0 and h in VEV else nc.scalar.copy
+                copy(rows[name, t][:, lo:hi], banks[h][:])
 
         last = TILES - 1
         fetched = {}
@@ -189,7 +196,7 @@ def tile_picked_edgecv_gelu_p_kernel(
                 nc.tensor.matmul(sums[:, b - b0], fetched[t, first, b], identity[:], start=(b == b0), stop=False, is_transpose=True)
             for b in range(b0, b1):
                 nc.tensor.matmul(sums[:, b - b0], fetched[t, second, b], identity[:], start=False, stop=(b == b1 - 1), is_transpose=True)
-            nc.scalar.activation(feats[:, t, d, b0 * P : b1 * P], sums[:].rearrange("p b i -> p (b i)"), GELU)
+            nc.scalar.activation(feats[:, t, d, b0 * P : b1 * P], sums[:].rearrange("p b i -> p (b i)"), GELU, bias=no_bias[:])
 
         z_row = sb.tile([P, BLOCKS * H], BF16, name="z_row")
         z_t = z_row[:].rearrange("p (r t c) -> p t r c", t=TILES, c=P // 2)
@@ -233,12 +240,13 @@ def tile_picked_edgecv_gelu_p_kernel(
 
         nc.vector.tensor_copy(x_scale[:], scale_table[:].indirect(offs_t[:]))
         pick_words(0, 0, S)
-        pick_words(1, 0, BANK)
         round_weight("e", 0, 0)
         quantize_weight("e", 0, 0, 1)
-        pick_words(1, BANK, S, "raw_e00")
+        pick_words(1, 0, BANK)
+        pick_words(1, *CUTS[1])
         round_weight("e", 0, 1)
         quantize_weight("e", 0, 1, 2)
+        pick_words(1, *CUTS[2], "raw_e01")
         project("e", 0)
         prepare("y", 0)
 

@@ -21,22 +21,21 @@ P = 128
 PACK = 4
 PASSES = K // (P * PACK)
 BANK = 512
+QUADRANTS = 4
+SCALE_ROWS = 4
+PER_COLUMN = 16
 TILES = H // P
-EDGES = 3
-LIST = 16
+LAST = TILES - 1
 BLOCKS = V // P
-ACC_BANKS = (0, 2, 0, 5, 0, 0, 0, 0)
+EDGES = 3
 CENTRE = EDGES
-VEV = (0,)
-CUTS = ((0, 512), (512, 768), (768, 1024))
-GP = ((0, 2), (2, 4))
-ZV = ()
-OV = ()
-CFIRST = 0
-SLOTS = (1, 3, 4, 6, 8, 10)
-HOLD = 1
-GELU_AT = {0: 11, 1: 13, 2: 15}
-PIECES = ((0, 1), (1, 2), (2, 3), (3, 4))
+LOOKUPS = EDGES + 1
+
+SPANS = ((0, BANK), (BANK, BANK + BANK // 2), (BANK + BANK // 2, S))
+HALVES = ((0, BLOCKS // 2), (BLOCKS // 2, BLOCKS))
+
+PRODUCT_BANK = 0
+SUM_BANKS = (2, 5)
 
 
 def tile_picked_edgecv_gelu_p_kernel(
@@ -48,6 +47,10 @@ def tile_picked_edgecv_gelu_p_kernel(
         sb = ctx.enter_context(tc.tile_pool(name="sb", bufs=1))
         psum = ctx.enter_context(tc.psum_pool(name="psum", bufs=1))
 
+        weights = {"e": w2, "y": w1}
+        products = [(name, t) for t in range(TILES) for name in ("ye" if t == LAST else "ey")]
+
+
         def load_list(src, name):
             dst = lists.tile(list(src.shape), U16, name=name)
             nc.sync.dma_start(dst[:], src)
@@ -55,45 +58,48 @@ def tile_picked_edgecv_gelu_p_kernel(
 
         def load_words(g):
             dst = sb.tile([P, T], U32, name=f"x_table{g}", align_bytes=64)
-            nc.sync.dma_start(dst[:].bitcast(I32), x_words[g].rearrange("p n t -> p (n t)").bitcast(I32))
+            nc.sync.dma_start(dst[:].bitcast(I32), x_words[g].rearrange("p n j -> p (n j)").bitcast(I32))
             return dst
 
-        weights = {"e": w2, "y": w1}
-        raw = {}
-        order = [(name, t) for t in range(TILES) for name in ("ye" if t == TILES - 1 else "ey")]
+        def raw_tag(k, g):
+            return f"raw{k}{g}"
 
-        def load_weight(name, t, g):
-            raw[name, t, g] = sb.tile([P, PACK, P], F32, name=f"raw_{name}{t}{g}", align_bytes=64)
-            rows = weights[name][g * P * PACK : (g + 1) * P * PACK, t * P : (t + 1) * P]
-            nc.sync.dma_start(raw[name, t, g][:], rows.rearrange("(p j) c -> p j c", j=PACK))
+        raw = {}
+
+        def load_weight(k, g):
+            name, t = products[k]
+            raw[k, g] = sb.tile([P, PACK, P], F32, name=raw_tag(k, g), align_bytes=64)
+            src = weights[name][g * P * PACK : (g + 1) * P * PACK, t * P : (t + 1) * P]
+            nc.sync.dma_start(raw[k, g][:], src.rearrange("(p j) c -> p j c", j=PACK))
 
         scale_table = sb.tile([P, T], U8, name="scale_table", align_bytes=64)
         nc.vector.memset(scale_table[:].bitcast(I32), 0)
         w3_scale = sb.tile([P, N], U8, name="w3_scale", align_bytes=64)
         nc.gpsimd.memset(w3_scale[:].bitcast(I32), 0)
 
-        offs_t = load_list(offs, "offs")
+        picked = load_list(offs, "offs")
         x_table = [load_words(0)]
-        for q in range(4):
+        for q in range(QUADRANTS):
             nc.sync.dma_start(
-                scale_table[32 * q : 32 * q + 4 * PASSES, :].bitcast(I32), x_scales[:, 4 * q : 4 * q + 4, :].bitcast(I32)
+                scale_table[32 * q : 32 * q + SCALE_ROWS * PASSES, :].bitcast(I32),
+                x_scales[:, SCALE_ROWS * q : SCALE_ROWS * (q + 1), :].bitcast(I32),
             )
-        load_weight("e", 0, 0)
+        load_weight(0, 0)
         x_table.append(load_words(1))
-        load_weight("e", 0, 1)
-        load_weight("y", 0, 0)
-        load_weight("y", 0, 1)
-        pos_t = [load_list(pos1, "pos1")]
-        pos_t.append(load_list(pos2, "pos2"))
-        pos_t.append(load_list(pos3, "pos3"))
-        cen_t = load_list(cen, "cen")
-        for name, t in order[2:]:
+        load_weight(0, 1)
+        load_weight(1, 0)
+        load_weight(1, 1)
+        places = [load_list(pos1, "pos1"), load_list(pos2, "pos2"), load_list(pos3, "pos3"), load_list(cen, "cen")]
+        for k in range(2, len(products)):
             for g in range(PASSES):
-                load_weight(name, t, g)
+                load_weight(k, g)
         w3_code = sb.tile([P, 2 * N], U8, name="w3_code", align_bytes=64)
         nc.sync.dma_start(w3_code[:].bitcast(I32), w3_words[0].bitcast(I32))
-        for q in range(4):
-            nc.sync.dma_start(w3_scale[32 * q : 32 * q + 4, :].bitcast(I32), w3_scales[0, 4 * q : 4 * q + 4, :].bitcast(I32))
+        for q in range(QUADRANTS):
+            nc.sync.dma_start(
+                w3_scale[32 * q : 32 * q + SCALE_ROWS, :].bitcast(I32),
+                w3_scales[0, SCALE_ROWS * q : SCALE_ROWS * (q + 1), :].bitcast(I32),
+            )
 
         identity = sb.tile([P, P], F32, name="identity")
         make_identity(nc, identity[:])
@@ -102,179 +108,201 @@ def tile_picked_edgecv_gelu_p_kernel(
         no_bias = sb.tile([P, 1], F32, name="no_bias")
         nc.scalar.activation(no_bias[:], zero[:], GELU)
 
+
         x_scale = sb.tile([P, S], U8, name="x_scale", align_bytes=64)
         x_code = [[] for g in range(PASSES)]
 
-        def pick_words(g, lo, hi, after=None):
-            name = f"x_code{g}{lo}"
-            dst = sb.tile([P, hi - lo], U32, name=name, tag=after or name, align_bytes=64)
-            nc.vector.tensor_copy(dst[:], x_table[g][:].indirect(offs_t[:, lo // LIST : hi // LIST]))
+        def entries(index, lo, hi):
+            return index[:, lo // PER_COLUMN : hi // PER_COLUMN]
+
+        def pick_words(g, lo, hi, tag):
+            dst = sb.tile([P, hi - lo], U32, name=f"x_code{g}_{lo}", tag=tag, align_bytes=64)
+            nc.vector.tensor_copy(dst[:], x_table[g][:].indirect(entries(picked, lo, hi)))
             x_code[g].append((lo, hi, dst))
+
 
         w_code, w_scale, w_bf = {}, {}, {}
 
-        def bf_tag(k):
-            return f"w_code_{order[k - 2][0]}{order[k - 2][1]}" if k >= 2 else f"w_bf{k}"
+        def code_tag(k):
+            return f"w_code{k}"
 
-        def round_weight(name, t, g):
+        def rounded_tag(k):
+            return code_tag(k - 2) if k >= 2 else f"w_bf{k}"
+
+        def round_weight(k, g):
             if g == 0:
-                w_bf[name, t] = sb.tile([P, PASSES, P, PACK], BF16, name=f"w_bf_{name}{t}", tag=bf_tag(order.index((name, t))), align_bytes=64)
-                w_code[name, t] = sb.tile([P, PASSES, P], U32, name=f"w_code_{name}{t}", align_bytes=64)
-                w_scale[name, t] = sb.tile([P, PASSES, P], U8, name=f"w_scale_{name}{t}", align_bytes=64)
+                w_bf[k] = sb.tile([P, PASSES, P, PACK], BF16, name=f"w_bf{k}", tag=rounded_tag(k), align_bytes=64)
+                w_code[k] = sb.tile([P, PASSES, P], U32, name=code_tag(k), align_bytes=64)
+                w_scale[k] = sb.tile([P, PASSES, P], U8, name=f"w_scale{k}", align_bytes=64)
             nc.scalar.copy(
-                w_bf[name, t][:, g].rearrange("p (u m e) j -> p m j u e", u=2, e=2),
-                raw[name, t, g][:].rearrange("p j (m u e) -> p m j u e", u=2, e=2),
+                w_bf[k][:, g].rearrange("p (u m e) j -> p m j u e", u=2, e=2),
+                raw[k, g][:].rearrange("p j (m u e) -> p m j u e", u=2, e=2),
             )
 
-        def quantize_weight(name, t, lo, hi):
+        def quantize_weight(k, g0, g1):
             nc.vector.quantize_mx(
-                out=w_code[name, t][:, lo:hi].rearrange("p g c -> p (g c)").bitcast(E4M3),
-                scales=w_scale[name, t][:, lo:hi].rearrange("p g c -> p (g c)"),
-                in_=w_bf[name, t][:, lo:hi].rearrange("p g c j -> p (g c j)"),
+                out=w_code[k][:, g0:g1].rearrange("p g c -> p (g c)").bitcast(E4M3),
+                scales=w_scale[k][:, g0:g1].rearrange("p g c -> p (g c)"),
+                in_=w_bf[k][:, g0:g1].rearrange("p g c j -> p (g c j)"),
             )
 
-        def prepare(name, t):
+        def prepare(k):
             for g in range(PASSES):
-                round_weight(name, t, g)
-            quantize_weight(name, t, 0, PASSES)
+                round_weight(k, g)
+            quantize_weight(k, 0, PASSES)
 
-        def bank(n):
-            return f"bank{n % 8}"
 
         rows = {}
 
-        def project(name, t):
-            k = order.index((name, t))
-            after = f"raw_{order[k + 1][0]}{order[k + 1][1]}0" if 0 < k < len(order) - 1 else f"rows_{name}{t}"
-            rows[name, t] = sb.tile([P, S], F32, name=f"rows_{name}{t}", tag=after, align_bytes=64)
-            spans = CUTS if k == 0 else ((0, BANK), (BANK, S))
-            banks = [psum.tile([P, hi - lo], F32, name=f"acc_{name}{t}{lo}", tag=bank((0, 1, 4)[h] if k == 0 else ACC_BANKS[k] + h)) for h, (lo, hi) in enumerate(spans)]
-            steps = [(g, h) for g in range(PASSES) for h in range(len(spans))]
-            if k > 0:
-                steps.sort(key=lambda s: s[1])
-            for g, h in steps:
-                lo, hi = spans[h]
-                parts = [(max(lo, a), min(hi, b), a, src) for a, b, src in x_code[g] if max(lo, a) < min(hi, b)]
-                for c0, c1, a, src in parts:
+        def bank(number):
+            return f"bank{number}"
+
+        def multiply(k, g, lo, hi, acc):
+            for first, end, words in x_code[g]:
+                c0, c1 = max(lo, first), min(hi, end)
+                if c0 < c1:
                     nc.tensor.matmul_mx(
-                        out=banks[h][:, c0 - lo : c1 - lo],
-                        lhsT=w_code[name, t][:, g].bitcast(E4M3),
-                        lhsT_scale=w_scale[name, t][:, g],
-                        rhs=src[:, c0 - a : c1 - a].bitcast(E4M3),
-                        rhs_scale=x_scale[4 * g :, c0:c1],
+                        out=acc[:, c0 - lo : c1 - lo],
+                        lhsT=w_code[k][:, g].bitcast(E4M3),
+                        lhsT_scale=w_scale[k][:, g],
+                        rhs=words[:, c0 - first : c1 - first].bitcast(E4M3),
+                        rhs_scale=x_scale[SCALE_ROWS * g :, c0:c1],
                         start=(g == 0),
                         stop=(g == PASSES - 1 and c1 == hi),
                     )
-            for h, (lo, hi) in enumerate(spans):
-                copy = nc.vector.tensor_copy if k == 0 and h in VEV else nc.scalar.copy
-                copy(rows[name, t][:, lo:hi], banks[h][:])
 
-        last = TILES - 1
+        def project_first():
+            dst = sb.tile([P, S], F32, name="rows0", align_bytes=64)
+            rows[products[0]] = dst
+            numbers = (PRODUCT_BANK, PRODUCT_BANK + 1, SUM_BANKS[0] + 2)
+            accs = [psum.tile([P, hi - lo], F32, name=f"acc0_{lo}", tag=bank(n)) for n, (lo, hi) in zip(numbers, SPANS)]
+            for g in range(PASSES):
+                for acc, (lo, hi) in zip(accs, SPANS):
+                    multiply(0, g, lo, hi, acc)
+            for acc, (lo, hi) in zip(accs, SPANS):
+                copy = nc.vector.tensor_copy if lo == 0 else nc.scalar.copy
+                copy(dst[:, lo:hi], acc[:])
+
+        def project(k):
+            name, t = products[k]
+            tag = raw_tag(k + 1, 0) if k + 1 < len(products) else f"rows{k}"
+            dst = sb.tile([P, S], F32, name=f"rows{k}", tag=tag, align_bytes=64)
+            rows[name, t] = dst
+            first = SUM_BANKS[t // 2] if name == "y" and t < LAST else PRODUCT_BANK
+            accs = [psum.tile([P, BANK], F32, name=f"acc{k}_{h}", tag=bank(first + h)) for h in range(S // BANK)]
+            for h, acc in enumerate(accs):
+                for g in range(PASSES):
+                    multiply(k, g, h * BANK, (h + 1) * BANK, acc)
+            for h, acc in enumerate(accs):
+                nc.scalar.copy(dst[:, h * BANK : (h + 1) * BANK], acc[:])
+
+
         fetched = {}
 
-        def fetch(t, d, b0, b1, after):
-            source, index = (rows["e", t], pos_t[d]) if d < EDGES else (rows["y", t], cen_t)
-            name = f"fetched{t}{d}{b0}"
-            dst = sb.tile([P, (b1 - b0) * P], F32, name=name, tag=after or name, align_bytes=64)
-            nc.vector.tensor_copy(dst[:], source[:].indirect(index[:, b0 * P // LIST : b1 * P // LIST]))
-            for b in range(b0, b1):
-                fetched[t, d, b] = dst[:, (b - b0) * P : (b - b0 + 1) * P]
-
-        def fetch_last():
-            dst = sb.tile([P, V], F32, name="fetched_last")
-            for b0, b1 in GP:
-                nc.vector.tensor_copy(dst[:, b0 * P : b1 * P], rows["e", last][:].indirect(pos_t[2][:, b0 * P // LIST : b1 * P // LIST]))
-            for b in range(BLOCKS):
-                fetched[last, 2, b] = dst[:, b * P : (b + 1) * P]
+        def fetch(t, d, dst, b0, b1):
+            fetched[t, d] = dst
+            source = rows["y" if d == CENTRE else "e", t]
+            nc.vector.tensor_copy(dst[:, b0 * P : b1 * P], source[:].indirect(entries(places[d], b0 * P, b1 * P)))
 
         feats = sb.tile([P, TILES, EDGES, V], BF16, name="feats")
 
-        def edge_features(t, d, b0, b1, where):
-            sums = psum.tile([P, b1 - b0, P], F32, name=f"sums{t}{d}{b0}", tag=bank(where))
-            first, second = (CENTRE, d) if d == EDGES - 1 or t == last or CFIRST else (d, CENTRE)
+        def edge_features(t, d, b0, b1, number):
+            sums = psum.tile([P, b1 - b0, P], F32, name=f"sums{t}{d}{b0}", tag=bank(number))
+            opens, adds = sorted((d, CENTRE), key=lambda look_up: lookup_order(t).index(look_up))
             for b in range(b0, b1):
-                nc.tensor.matmul(sums[:, b - b0], fetched[t, first, b], identity[:], start=(b == b0), stop=False, is_transpose=True)
+                block = fetched[t, opens][:, b * P : (b + 1) * P]
+                nc.tensor.matmul(sums[:, b - b0], block, identity[:], start=(b == b0), stop=False, is_transpose=True)
             for b in range(b0, b1):
-                nc.tensor.matmul(sums[:, b - b0], fetched[t, second, b], identity[:], start=False, stop=(b == b1 - 1), is_transpose=True)
-            nc.scalar.activation(feats[:, t, d, b0 * P : b1 * P], sums[:].rearrange("p b i -> p (b i)"), GELU, bias=no_bias[:])
+                block = fetched[t, adds][:, b * P : (b + 1) * P]
+                nc.tensor.matmul(sums[:, b - b0], block, identity[:], start=False, stop=(b == b1 - 1), is_transpose=True)
+            nc.scalar.activation(feats[:, t, d, b0 * P : b1 * P], sums[:].rearrange("p b c -> p (b c)"), GELU, bias=no_bias[:])
+
+        def lookup_order(t):
+            return (CENTRE, 0, 1, 2) if t == LAST else (0, 1, CENTRE, 2)
+
 
         z_row = sb.tile([P, BLOCKS * H], BF16, name="z_row")
-        z_t = z_row[:].rearrange("p (r t c) -> p t r c", t=TILES, c=P // 2)
+        z_runs = z_row[:].rearrange("p (r t c) -> p t r c", t=TILES, c=P // 2)
         pair = sb.tile([P, TILES, V], BF16, name="pair")
 
-        def larger(t0, t1):
+        def larger_of_two(t0, t1):
             nc.vector.tensor_tensor(pair[:, t0:t1], feats[:, t0:t1, 0], feats[:, t0:t1, 1], MAX)
 
-        def largest(t0, t1, b0, b1):
-            cols = slice(b0 * P, b1 * P)
+        def finish(b, turned_bank, out_bank):
+            cols = slice(b * P, (b + 1) * P)
             nc.vector.tensor_tensor(
-                z_t[:, t0:t1, 2 * b0 : 2 * b1],
-                pair[:, t0:t1, cols].rearrange("p t (r c) -> p t r c", c=P // 2),
-                feats[:, t0:t1, 2, cols].rearrange("p t (r c) -> p t r c", c=P // 2),
+                z_runs[:, :, 2 * b : 2 * (b + 1)],
+                pair[:, :, cols].rearrange("p t (u c) -> p t u c", u=2),
+                feats[:, :, 2, cols].rearrange("p t (u c) -> p t u c", u=2),
                 MAX,
             )
-
-        def finish(b0, b1):
-            nb = b1 - b0
-            words = z_row[:, b0 * H : b1 * H].bitcast(F32)
-            turned = psum.tile([P, nb, 2, P], F32, name=f"turned{b0}", tag=bank((3, 4, 0, 1)[b0]))
-            for b in range(nb):
-                for u in range(2):
-                    r = 2 * b + u
-                    nc.tensor.transpose(turned[:, b, u], words[:, r * P : (r + 1) * P], identity[:])
-            z_bf = sb.tile([P, nb, P, PACK], BF16, name=f"z_bf{b0}", align_bytes=64)
-            copy = nc.vector.tensor_copy if b0 in ZV else nc.scalar.copy
-            copy(z_bf[:].bitcast(F32), turned[:].rearrange("p b u v -> p b v u"))
-            z_code = sb.tile([P, nb * P], U32, name=f"z_code{b0}", align_bytes=64)
-            z_scale = sb.tile([P, nb * P], U8, name=f"z_scale{b0}", align_bytes=64)
-            nc.vector.quantize_mx(out=z_code[:].bitcast(E4M3), scales=z_scale[:], in_=z_bf[:].rearrange("p b v j -> p (b v j)"))
-            acc = psum.tile([P, nb * P], F32, name=f"out{b0}", tag=bank((5, 6, 7, 2)[b0]))
+            words = z_row[:, b * H : (b + 1) * H].bitcast(F32)
+            turned = psum.tile([P, 2, P], F32, name=f"turned{b}", tag=bank(turned_bank))
+            for u in range(2):
+                nc.tensor.transpose(turned[:, u], words[:, u * P : (u + 1) * P], identity[:])
+            z_bf = sb.tile([P, P, PACK], BF16, name=f"z_bf{b}", align_bytes=64)
+            nc.scalar.copy(z_bf[:].bitcast(F32), turned[:].rearrange("p u v -> p v u"))
+            z_code = sb.tile([P, P], U32, name=f"z_code{b}", align_bytes=64)
+            z_scale = sb.tile([P, P], U8, name=f"z_scale{b}", align_bytes=64)
+            nc.vector.quantize_mx(out=z_code[:].bitcast(E4M3), scales=z_scale[:], in_=z_bf[:].rearrange("p v j -> p (v j)"))
+            acc = psum.tile([P, P], F32, name=f"out{b}", tag=bank(out_bank))
             nc.tensor.matmul_mx(
-                out=acc[:], lhsT=w3_code[:].bitcast(E2M1), lhsT_scale=w3_scale[:],
-                rhs=z_code[:].bitcast(E4M3), rhs_scale=z_scale[:], start=True, stop=True,
+                out=acc[:],
+                lhsT=w3_code[:].bitcast(E2M1),
+                lhsT_scale=w3_scale[:],
+                rhs=z_code[:].bitcast(E4M3),
+                rhs_scale=z_scale[:],
+                start=True,
+                stop=True,
             )
-            result = sb.tile([P, nb * P], F32, name=f"result{b0}")
-            copy = nc.vector.tensor_copy if b0 in OV else nc.scalar.copy
-            copy(result[:], acc[:])
-            nc.sync.dma_start(out[:, b0 * P : b1 * P], result[:])
+            result = sb.tile([P, P], F32, name=f"result{b}")
+            nc.scalar.copy(result[:], acc[:])
+            nc.sync.dma_start(out[:, cols], result[:])
 
-        nc.vector.tensor_copy(x_scale[:], scale_table[:].indirect(offs_t[:]))
-        pick_words(0, 0, S)
-        round_weight("e", 0, 0)
-        quantize_weight("e", 0, 0, 1)
-        pick_words(1, 0, BANK)
-        pick_words(1, *CUTS[1])
-        round_weight("e", 0, 1)
-        quantize_weight("e", 0, 1, 2)
-        pick_words(1, *CUTS[2], "raw_e01")
-        project("e", 0)
-        prepare("y", 0)
 
-        for n in range(4 * TILES - 1):
-            t, d = n // 4, ((0, 1, CENTRE, 2) if n // 4 < last else (CENTRE, 0, 1))[n % 4]
-            after = None
-            if n in SLOTS:
-                k = SLOTS.index(n) + 2
-                prepare(*order[k])
-                project(*order[k - 1])
-                after = f"raw_{order[k][0]}{order[k][1]}1"
-            elif HOLD and n - 1 in SLOTS:
-                after = bf_tag(SLOTS.index(n - 1) + 2)
-            if n == SLOTS[-1] + 1:
-                project(*order[-1])
-            fetch(t, d, 0, BLOCKS, after)
-            for s in range(last):
-                if GELU_AT[s] == n + 1:
-                    for e in range(EDGES):
-                        edge_features(s, e, 0, BLOCKS, (2, 5, 2)[s] + e)
-                    if s == last - 1:
-                        larger(0, last)
-        edge_features(last, 0, 0, BLOCKS, 0)
-        edge_features(last, 1, 0, BLOCKS, 1)
-        fetch_last()
-        for n, (b0, b1) in enumerate(GP):
-            edge_features(last, 2, b0, b1, (5, 6, 7, 2)[n])
-        larger(last, TILES)
-        for b0, b1 in PIECES:
-            largest(0, TILES, b0, b1)
-            finish(b0, b1)
+        nc.vector.tensor_copy(x_scale[:], scale_table[:].indirect(picked[:]))
+        pick_words(0, 0, S, "x_code0")
+        round_weight(0, 0)
+        quantize_weight(0, 0, 1)
+        pick_words(1, *SPANS[0], "x_code1a")
+        pick_words(1, *SPANS[1], "x_code1b")
+        round_weight(0, 1)
+        quantize_weight(0, 1, 2)
+        pick_words(1, *SPANS[2], raw_tag(0, 1))
+        project_first()
+        prepare(1)
+
+        ahead_of = {2 * k - (4 if products[k][1] == LAST else 3): k for k in range(2, len(products))}
+        last_prepared = max(ahead_of)
+        for n in range(LOOKUPS * TILES - 1):
+            t, d = n // LOOKUPS, lookup_order(n // LOOKUPS)[n % LOOKUPS]
+            tag = f"fetched{t}{d}"
+            if n in ahead_of:
+                k = ahead_of[n]
+                prepare(k)
+                project(k - 1)
+                tag = raw_tag(k, 1)
+            elif n - 1 in ahead_of:
+                tag = rounded_tag(ahead_of[n - 1])
+            if n == last_prepared + 1:
+                project(len(products) - 1)
+            fetch(t, d, sb.tile([P, V], F32, name=f"fetched{t}{d}", tag=tag, align_bytes=64), 0, BLOCKS)
+            if n >= last_prepared and (n - last_prepared) % 2 == 0:
+                done = (n - last_prepared) // 2
+                for edge in range(EDGES):
+                    edge_features(done, edge, 0, BLOCKS, SUM_BANKS[done % 2] + edge)
+        larger_of_two(0, LAST)
+
+        for edge in range(EDGES - 1):
+            edge_features(LAST, edge, 0, BLOCKS, PRODUCT_BANK + edge)
+        last_fetched = sb.tile([P, V], F32, name="last_fetched")
+        for b0, b1 in HALVES:
+            fetch(LAST, EDGES - 1, last_fetched, b0, b1)
+        for half, (b0, b1) in enumerate(HALVES):
+            edge_features(LAST, EDGES - 1, b0, b1, SUM_BANKS[1] + half)
+        larger_of_two(LAST, TILES)
+
+        turned_banks = (SUM_BANKS[0] + 1, SUM_BANKS[0] + 2, PRODUCT_BANK, PRODUCT_BANK + 1)
+        out_banks = (SUM_BANKS[1], SUM_BANKS[1] + 1, SUM_BANKS[1] + 2, SUM_BANKS[0])
+        for b in range(BLOCKS):
+            finish(b, turned_banks[b], out_banks[b])

@@ -21,7 +21,7 @@ P = 128
 PACK = 4
 PASSES = K // (P * PACK)
 BANK = 512
-QUADRANTS = 4
+QUADRANT = 32
 SCALE_ROWS = 4
 PER_COLUMN = 16
 TILES = H // P
@@ -61,16 +61,16 @@ def tile_picked_edgecv_gelu_p_kernel(
             nc.sync.dma_start(dst[:].bitcast(I32), x_words[g].rearrange("p n j -> p (n j)").bitcast(I32))
             return dst
 
-        def raw_tag(k, g):
-            return f"raw{k}{g}"
+        def raw_tag(prod, g):
+            return f"raw{prod}{g}"
 
         raw = {}
 
-        def load_weight(k, g):
-            name, t = products[k]
-            raw[k, g] = sb.tile([P, PACK, P], F32, name=raw_tag(k, g), align_bytes=64)
+        def load_weight(prod, g):
+            name, t = products[prod]
+            raw[prod, g] = sb.tile([P, PACK, P], F32, name=raw_tag(prod, g), align_bytes=64)
             src = weights[name][g * P * PACK : (g + 1) * P * PACK, t * P : (t + 1) * P]
-            nc.sync.dma_start(raw[k, g][:], src.rearrange("(p j) c -> p j c", j=PACK))
+            nc.sync.dma_start(raw[prod, g][:], src.rearrange("(p j) c -> p j c", j=PACK))
 
         scale_table = sb.tile([P, T], U8, name="scale_table", align_bytes=64)
         nc.vector.memset(scale_table[:].bitcast(I32), 0)
@@ -78,26 +78,27 @@ def tile_picked_edgecv_gelu_p_kernel(
         nc.gpsimd.memset(w3_scale[:].bitcast(I32), 0)
 
         picked = load_list(offs, "offs")
-        x_table = [load_words(0)]
-        for q in range(QUADRANTS):
+        places = [load_list(pos1, "pos1")]
+        for q in range(P // QUADRANT):
             nc.sync.dma_start(
-                scale_table[32 * q : 32 * q + SCALE_ROWS * PASSES, :].bitcast(I32),
+                scale_table[QUADRANT * q : QUADRANT * q + SCALE_ROWS * PASSES, :].bitcast(I32),
                 x_scales[:, SCALE_ROWS * q : SCALE_ROWS * (q + 1), :].bitcast(I32),
             )
+        x_table = [load_words(0)]
         load_weight(0, 0)
         x_table.append(load_words(1))
         load_weight(0, 1)
         load_weight(1, 0)
         load_weight(1, 1)
-        places = [load_list(pos1, "pos1"), load_list(pos2, "pos2"), load_list(pos3, "pos3"), load_list(cen, "cen")]
-        for k in range(2, len(products)):
+        places.extend([load_list(pos2, "pos2"), load_list(pos3, "pos3"), load_list(cen, "cen")])
+        for prod in range(2, len(products)):
             for g in range(PASSES):
-                load_weight(k, g)
+                load_weight(prod, g)
         w3_code = sb.tile([P, 2 * N], U8, name="w3_code", align_bytes=64)
         nc.sync.dma_start(w3_code[:].bitcast(I32), w3_words[0].bitcast(I32))
-        for q in range(QUADRANTS):
+        for q in range(P // QUADRANT):
             nc.sync.dma_start(
-                w3_scale[32 * q : 32 * q + SCALE_ROWS, :].bitcast(I32),
+                w3_scale[QUADRANT * q : QUADRANT * q + SCALE_ROWS, :].bitcast(I32),
                 w3_scales[0, SCALE_ROWS * q : SCALE_ROWS * (q + 1), :].bitcast(I32),
             )
 
@@ -123,33 +124,33 @@ def tile_picked_edgecv_gelu_p_kernel(
 
         w_code, w_scale, w_bf = {}, {}, {}
 
-        def code_tag(k):
-            return f"w_code{k}"
+        def code_tag(prod):
+            return f"w_code{prod}"
 
-        def rounded_tag(k):
-            return code_tag(k - 2) if k >= 2 else f"w_bf{k}"
+        def rounded_tag(prod):
+            return code_tag(prod - 2) if prod >= 2 else f"w_bf{prod}"
 
-        def round_weight(k, g):
+        def round_weight(prod, g):
             if g == 0:
-                w_bf[k] = sb.tile([P, PASSES, P, PACK], BF16, name=f"w_bf{k}", tag=rounded_tag(k), align_bytes=64)
-                w_code[k] = sb.tile([P, PASSES, P], U32, name=code_tag(k), align_bytes=64)
-                w_scale[k] = sb.tile([P, PASSES, P], U8, name=f"w_scale{k}", align_bytes=64)
+                w_bf[prod] = sb.tile([P, PASSES, P, PACK], BF16, name=f"w_bf{prod}", tag=rounded_tag(prod), align_bytes=64)
+                w_code[prod] = sb.tile([P, PASSES, P], U32, name=code_tag(prod), align_bytes=64)
+                w_scale[prod] = sb.tile([P, PASSES, P], U8, name=f"w_scale{prod}", align_bytes=64)
             nc.scalar.copy(
-                w_bf[k][:, g].rearrange("p (u m e) j -> p m j u e", u=2, e=2),
-                raw[k, g][:].rearrange("p j (m u e) -> p m j u e", u=2, e=2),
+                w_bf[prod][:, g].rearrange("p (u m o) j -> p m j u o", u=2, o=2),
+                raw[prod, g][:].rearrange("p j (m u o) -> p m j u o", u=2, o=2),
             )
 
-        def quantize_weight(k, g0, g1):
+        def quantize_weight(prod, g0, g1):
             nc.vector.quantize_mx(
-                out=w_code[k][:, g0:g1].rearrange("p g c -> p (g c)").bitcast(E4M3),
-                scales=w_scale[k][:, g0:g1].rearrange("p g c -> p (g c)"),
-                in_=w_bf[k][:, g0:g1].rearrange("p g c j -> p (g c j)"),
+                out=w_code[prod][:, g0:g1].rearrange("p g c -> p (g c)").bitcast(E4M3),
+                scales=w_scale[prod][:, g0:g1].rearrange("p g c -> p (g c)"),
+                in_=w_bf[prod][:, g0:g1].rearrange("p g c j -> p (g c j)"),
             )
 
-        def prepare(k):
+        def prepare(prod):
             for g in range(PASSES):
-                round_weight(k, g)
-            quantize_weight(k, 0, PASSES)
+                round_weight(prod, g)
+            quantize_weight(prod, 0, PASSES)
 
 
         rows = {}
@@ -157,14 +158,14 @@ def tile_picked_edgecv_gelu_p_kernel(
         def bank(number):
             return f"bank{number}"
 
-        def multiply(k, g, lo, hi, acc):
+        def multiply(prod, g, lo, hi, acc):
             for first, end, words in x_code[g]:
                 c0, c1 = max(lo, first), min(hi, end)
                 if c0 < c1:
                     nc.tensor.matmul_mx(
                         out=acc[:, c0 - lo : c1 - lo],
-                        lhsT=w_code[k][:, g].bitcast(E4M3),
-                        lhsT_scale=w_scale[k][:, g],
+                        lhsT=w_code[prod][:, g].bitcast(E4M3),
+                        lhsT_scale=w_scale[prod][:, g],
                         rhs=words[:, c0 - first : c1 - first].bitcast(E4M3),
                         rhs_scale=x_scale[SCALE_ROWS * g :, c0:c1],
                         start=(g == 0),
@@ -175,7 +176,7 @@ def tile_picked_edgecv_gelu_p_kernel(
             dst = sb.tile([P, S], F32, name="rows0", align_bytes=64)
             rows[products[0]] = dst
             numbers = (PRODUCT_BANK, PRODUCT_BANK + 1, SUM_BANKS[0] + 2)
-            accs = [psum.tile([P, hi - lo], F32, name=f"acc0_{lo}", tag=bank(n)) for n, (lo, hi) in zip(numbers, SPANS)]
+            accs = [psum.tile([P, hi - lo], F32, name=f"acc0_{lo}", tag=bank(number)) for number, (lo, hi) in zip(numbers, SPANS)]
             for g in range(PASSES):
                 for acc, (lo, hi) in zip(accs, SPANS):
                     multiply(0, g, lo, hi, acc)
@@ -183,21 +184,24 @@ def tile_picked_edgecv_gelu_p_kernel(
                 copy = nc.vector.tensor_copy if lo == 0 else nc.scalar.copy
                 copy(dst[:, lo:hi], acc[:])
 
-        def project(k):
-            name, t = products[k]
-            tag = raw_tag(k + 1, 0) if k + 1 < len(products) else f"rows{k}"
-            dst = sb.tile([P, S], F32, name=f"rows{k}", tag=tag, align_bytes=64)
+        def project(prod):
+            name, t = products[prod]
+            tag = raw_tag(prod + 1, 0) if prod + 1 < len(products) else f"rows{prod}"
+            dst = sb.tile([P, S], F32, name=f"rows{prod}", tag=tag, align_bytes=64)
             rows[name, t] = dst
-            first = SUM_BANKS[t // 2] if name == "y" and t < LAST else PRODUCT_BANK
-            accs = [psum.tile([P, BANK], F32, name=f"acc{k}_{h}", tag=bank(first + h)) for h in range(S // BANK)]
+            number = SUM_BANKS[t] if name == "y" and t < len(SUM_BANKS) else PRODUCT_BANK
+            accs = [psum.tile([P, BANK], F32, name=f"acc{prod}_{h}", tag=bank(number + h)) for h in range(S // BANK)]
             for h, acc in enumerate(accs):
                 for g in range(PASSES):
-                    multiply(k, g, h * BANK, (h + 1) * BANK, acc)
+                    multiply(prod, g, h * BANK, (h + 1) * BANK, acc)
             for h, acc in enumerate(accs):
                 nc.scalar.copy(dst[:, h * BANK : (h + 1) * BANK], acc[:])
 
 
         fetched = {}
+
+        def lookup_order(t):
+            return (CENTRE, 0, 1, 2) if t == LAST else (0, 1, CENTRE, 2)
 
         def fetch(t, d, dst, b0, b1):
             fetched[t, d] = dst
@@ -216,9 +220,6 @@ def tile_picked_edgecv_gelu_p_kernel(
                 block = fetched[t, adds][:, b * P : (b + 1) * P]
                 nc.tensor.matmul(sums[:, b - b0], block, identity[:], start=False, stop=(b == b1 - 1), is_transpose=True)
             nc.scalar.activation(feats[:, t, d, b0 * P : b1 * P], sums[:].rearrange("p b c -> p (b c)"), GELU, bias=no_bias[:])
-
-        def lookup_order(t):
-            return (CENTRE, 0, 1, 2) if t == LAST else (0, 1, CENTRE, 2)
 
 
         z_row = sb.tile([P, BLOCKS * H], BF16, name="z_row")
@@ -272,16 +273,16 @@ def tile_picked_edgecv_gelu_p_kernel(
         project_first()
         prepare(1)
 
-        ahead_of = {2 * k - (4 if products[k][1] == LAST else 3): k for k in range(2, len(products))}
+        ahead_of = {2 * prod - (3 if products[prod][1] == 1 else 4): prod for prod in range(2, len(products))}
         last_prepared = max(ahead_of)
         for n in range(LOOKUPS * TILES - 1):
             t, d = n // LOOKUPS, lookup_order(n // LOOKUPS)[n % LOOKUPS]
             tag = f"fetched{t}{d}"
             if n in ahead_of:
-                k = ahead_of[n]
-                prepare(k)
-                project(k - 1)
-                tag = raw_tag(k, 1)
+                prod = ahead_of[n]
+                prepare(prod)
+                project(prod - 1)
+                tag = raw_tag(prod, 1)
             elif n - 1 in ahead_of:
                 tag = rounded_tag(ahead_of[n - 1])
             if n == last_prepared + 1:
@@ -290,7 +291,7 @@ def tile_picked_edgecv_gelu_p_kernel(
             if n >= last_prepared and (n - last_prepared) % 2 == 0:
                 done = (n - last_prepared) // 2
                 for edge in range(EDGES):
-                    edge_features(done, edge, 0, BLOCKS, SUM_BANKS[done % 2] + edge)
+                    edge_features(done, edge, 0, BLOCKS, SUM_BANKS[done % len(SUM_BANKS)] + edge)
         larger_of_two(0, LAST)
 
         for edge in range(EDGES - 1):

@@ -15,6 +15,7 @@ U8 = mybir.dt.uint8
 E4M3 = mybir.dt.float8_e4m3fn_x4
 E2M1 = mybir.dt.float4_e2m1fn_x4
 GELU = mybir.ActivationFunctionType.Gelu_apprx_tanh
+COPY = mybir.ActivationFunctionType.Copy
 MAX = mybir.AluOpType.max
 
 P = 128
@@ -35,6 +36,11 @@ SPANS = ((0, BANK), (BANK, BANK + BANK // 2), (BANK + BANK // 2, S))
 HALVES = ((0, BLOCKS // 2), (BLOCKS // 2, BLOCKS))
 
 PRODUCT_BANK = 0
+PRODUCT_BANKS = (0, 2, 0, 2, 4, 2, 0, 2)
+ROUNDED_ON_VECTOR = (3, 6, 7)
+ON_SCALAR = ((2, CENTRE), (LAST, CENTRE))
+ROUNDED_TAG = {3: "raw21", 4: "w_code1", 5: "w_code2", 6: "w_code2", 7: "w_code2"}
+ROWS_TAG = {1: "raw20", 2: "raw40", 3: "raw50"}
 SUM_BANKS = (2, 5)
 
 
@@ -128,6 +134,8 @@ def tile_picked_edgecv_gelu_p_kernel(
             return f"w_code{prod}"
 
         def rounded_tag(prod):
+            if prod in ROUNDED_TAG:
+                return ROUNDED_TAG[prod]
             return code_tag(prod - 2) if prod >= 2 else f"w_bf{prod}"
 
         def round_weight(prod, g):
@@ -135,7 +143,8 @@ def tile_picked_edgecv_gelu_p_kernel(
                 w_bf[prod] = sb.tile([P, PASSES, P, PACK], BF16, name=f"w_bf{prod}", tag=rounded_tag(prod), align_bytes=64)
                 w_code[prod] = sb.tile([P, PASSES, P], U32, name=code_tag(prod), align_bytes=64)
                 w_scale[prod] = sb.tile([P, PASSES, P], U8, name=f"w_scale{prod}", align_bytes=64)
-            nc.scalar.copy(
+            copy = nc.vector.tensor_copy if prod in ROUNDED_ON_VECTOR else nc.scalar.copy
+            copy(
                 w_bf[prod][:, g].rearrange("p (u m o) j -> p m j u o", u=2, o=2),
                 raw[prod, g][:].rearrange("p j (m u o) -> p m j u o", u=2, o=2),
             )
@@ -186,10 +195,10 @@ def tile_picked_edgecv_gelu_p_kernel(
 
         def project(prod):
             name, t = products[prod]
-            tag = raw_tag(prod + 1, 0) if prod + 1 < len(products) else f"rows{prod}"
+            tag = ROWS_TAG.get(prod, f"rows{prod}")
             dst = sb.tile([P, S], F32, name=f"rows{prod}", tag=tag, align_bytes=64)
             rows[name, t] = dst
-            number = SUM_BANKS[t] if name == "y" and t < len(SUM_BANKS) else PRODUCT_BANK
+            number = PRODUCT_BANKS[prod]
             accs = [psum.tile([P, BANK], F32, name=f"acc{prod}_{h}", tag=bank(number + h)) for h in range(S // BANK)]
             for h, acc in enumerate(accs):
                 for g in range(PASSES):
@@ -203,10 +212,14 @@ def tile_picked_edgecv_gelu_p_kernel(
         def lookup_order(t):
             return (CENTRE, 0, 1, 2) if t == LAST else (0, 1, CENTRE, 2)
 
-        def fetch(t, d, dst, b0, b1):
+        def fetch(t, d, dst, b0, b1, on_scalar=False):
             fetched[t, d] = dst
             source = rows["y" if d == CENTRE else "e", t]
-            nc.vector.tensor_copy(dst[:, b0 * P : b1 * P], source[:].indirect(entries(places[d], b0 * P, b1 * P)))
+            looked_up = source[:].indirect(entries(places[d], b0 * P, b1 * P))
+            if on_scalar or (t, d) in ON_SCALAR:
+                nc.scalar.activation(dst[:, b0 * P : b1 * P], looked_up, COPY)
+            else:
+                nc.vector.tensor_copy(dst[:, b0 * P : b1 * P], looked_up)
 
         feats = sb.tile([P, TILES, EDGES, V], BF16, name="feats")
 
@@ -229,20 +242,23 @@ def tile_picked_edgecv_gelu_p_kernel(
         def larger_of_two(t0, t1):
             nc.vector.tensor_tensor(pair[:, t0:t1], feats[:, t0:t1, 0], feats[:, t0:t1, 1], MAX)
 
-        def finish(b, turned_bank, out_bank):
-            cols = slice(b * P, (b + 1) * P)
+        def largest(t0, t1, b0, b1):
+            cols = slice(b0 * P, b1 * P)
             nc.vector.tensor_tensor(
-                z_runs[:, :, 2 * b : 2 * (b + 1)],
-                pair[:, :, cols].rearrange("p t (u c) -> p t u c", u=2),
-                feats[:, :, 2, cols].rearrange("p t (u c) -> p t u c", u=2),
+                z_runs[:, t0:t1, 2 * b0 : 2 * b1],
+                pair[:, t0:t1, cols].rearrange("p t (r c) -> p t r c", c=P // 2),
+                feats[:, t0:t1, 2, cols].rearrange("p t (r c) -> p t r c", c=P // 2),
                 MAX,
             )
+
+        def finish(b, turned_bank, out_bank, copy=nc.scalar.copy):
+            cols = slice(b * P, (b + 1) * P)
             words = z_row[:, b * H : (b + 1) * H].bitcast(F32)
             turned = psum.tile([P, 2, P], F32, name=f"turned{b}", tag=bank(turned_bank))
             for u in range(2):
                 nc.tensor.transpose(turned[:, u], words[:, u * P : (u + 1) * P], identity[:])
             z_bf = sb.tile([P, P, PACK], BF16, name=f"z_bf{b}", align_bytes=64)
-            nc.scalar.copy(z_bf[:].bitcast(F32), turned[:].rearrange("p u v -> p v u"))
+            copy(z_bf[:].bitcast(F32), turned[:].rearrange("p u v -> p v u"))
             z_code = sb.tile([P, P], U32, name=f"z_code{b}", align_bytes=64)
             z_scale = sb.tile([P, P], U8, name=f"z_scale{b}", align_bytes=64)
             nc.vector.quantize_mx(out=z_code[:].bitcast(E4M3), scales=z_scale[:], in_=z_bf[:].rearrange("p v j -> p (v j)"))
@@ -273,37 +289,67 @@ def tile_picked_edgecv_gelu_p_kernel(
         project_first()
         prepare(1)
 
-        ahead_of = {2 * prod - (3 if products[prod][1] == 1 else 4): prod for prod in range(2, len(products))}
-        last_prepared = max(ahead_of)
-        for n in range(LOOKUPS * TILES - 1):
-            t, d = n // LOOKUPS, lookup_order(n // LOOKUPS)[n % LOOKUPS]
-            tag = f"fetched{t}{d}"
-            if n in ahead_of:
-                prod = ahead_of[n]
-                prepare(prod)
-                project(prod - 1)
-                tag = raw_tag(prod, 1)
-            elif n - 1 in ahead_of:
-                tag = rounded_tag(ahead_of[n - 1])
-            if n == last_prepared + 1:
-                project(len(products) - 1)
-            fetch(t, d, sb.tile([P, V], F32, name=f"fetched{t}{d}", tag=tag, align_bytes=64), 0, BLOCKS)
-            if n >= last_prepared and (n - last_prepared) % 2 == 0:
-                done = (n - last_prepared) // 2
-                for edge in range(EDGES):
-                    edge_features(done, edge, 0, BLOCKS, SUM_BANKS[done % len(SUM_BANKS)] + edge)
-        larger_of_two(0, LAST)
+        def look_up(t, d, tag=None):
+            fetch(t, d, sb.tile([P, V], F32, name=f"fetched{t}{d}", tag=tag or f"fetched{t}{d}", align_bytes=64), 0, BLOCKS)
 
-        for edge in range(EDGES - 1):
-            edge_features(LAST, edge, 0, BLOCKS, PRODUCT_BANK + edge)
+        def round_both(prod):
+            for g in range(PASSES):
+                round_weight(prod, g)
+
+        look_up(0, 0)
+        prepare(2)
+        project(1)
+        round_both(3)
+        look_up(0, 1, rounded_tag(2))
+        quantize_weight(3, 0, PASSES)
+        look_up(0, 2, raw_tag(3, 1))
+        prepare(4)
+        look_up(0, CENTRE, raw_tag(4, 1))
+        project(2)
+        prepare(5)
+        look_up(1, 0, raw_tag(5, 1))
+        project(3)
+        round_both(6)
+        look_up(1, 1, raw_tag(6, 0))
+        quantize_weight(6, 0, PASSES)
+        look_up(1, CENTRE)
+        round_both(7)
+        look_up(1, 2, raw_tag(7, 0))
+        quantize_weight(7, 0, PASSES)
         last_fetched = sb.tile([P, V], F32, name="last_fetched")
-        for b0, b1 in HALVES:
-            fetch(LAST, EDGES - 1, last_fetched, b0, b1)
-        for half, (b0, b1) in enumerate(HALVES):
-            edge_features(LAST, EDGES - 1, b0, b1, SUM_BANKS[1] + half)
-        larger_of_two(LAST, TILES)
-
-        turned_banks = (SUM_BANKS[0] + 1, SUM_BANKS[0] + 2, PRODUCT_BANK, PRODUCT_BANK + 1)
-        out_banks = (SUM_BANKS[1], SUM_BANKS[1] + 1, SUM_BANKS[1] + 2, SUM_BANKS[0])
-        for b in range(BLOCKS):
-            finish(b, turned_banks[b], out_banks[b])
+        project(4)
+        look_up(2, 0)
+        look_up(2, 1)
+        look_up(2, 2)
+        project(5)
+        edge_features(0, 0, 0, 4, 6)
+        look_up(2, CENTRE)
+        edge_features(0, 1, 0, 4, 4)
+        project(6)
+        edge_features(0, 2, 0, 4, 5)
+        look_up(3, CENTRE)
+        edge_features(1, 2, 0, 4, 6)
+        project(7)
+        edge_features(1, 0, 0, 4, 4)
+        fetch(LAST, EDGES - 1, last_fetched, 0, 2, on_scalar=True)
+        edge_features(1, 1, 0, 4, 5)
+        edge_features(2, 0, 0, 4, 7)
+        edge_features(2, 1, 0, 4, 0)
+        look_up(3, 0)
+        look_up(3, 1)
+        fetch(LAST, EDGES - 1, last_fetched, 2, 4)
+        edge_features(2, 2, 0, 4, 1)
+        larger_of_two(0, 3)
+        edge_features(3, 0, 0, 4, 6)
+        edge_features(3, 1, 0, 4, 4)
+        edge_features(3, 2, 0, 2, 2)
+        edge_features(3, 2, 2, 4, 3)
+        larger_of_two(3, 4)
+        largest(0, 4, 0, 1)
+        largest(0, 4, 1, 2)
+        largest(0, 4, 2, 3)
+        largest(0, 4, 3, 4)
+        finish(0, 5, 6)
+        finish(1, 7, 4)
+        finish(2, 0, 2)
+        finish(3, 1, 3)

@@ -143,11 +143,16 @@ def tile_picked_edgecv_gelu_p_kernel(
                 w_bf[prod] = sb.tile([P, PASSES, P, PACK], BF16, name=f"w_bf{prod}", tag=rounded_tag(prod), align_bytes=64)
                 w_code[prod] = sb.tile([P, PASSES, P], U32, name=code_tag(prod), align_bytes=64)
                 w_scale[prod] = sb.tile([P, PASSES, P], U8, name=f"w_scale{prod}", align_bytes=64)
-            copy = nc.vector.tensor_copy if prod in ROUNDED_ON_VECTOR else nc.scalar.copy
-            copy(
-                w_bf[prod][:, g].rearrange("p (u m o) j -> p m j u o", u=2, o=2),
-                raw[prod, g][:].rearrange("p j (m u o) -> p m j u o", u=2, o=2),
-            )
+            if prod in ROUNDED_ON_VECTOR:
+                nc.vector.tensor_copy(
+                    w_bf[prod][:, g].rearrange("p (u m o) j -> p m u o j", u=2, o=2),
+                    raw[prod, g][:].rearrange("p j (m u o) -> p m u o j", u=2, o=2),
+                )
+            else:
+                nc.scalar.copy(
+                    w_bf[prod][:, g].rearrange("p (u m o) j -> p m j u o", u=2, o=2),
+                    raw[prod, g][:].rearrange("p j (m u o) -> p m j u o", u=2, o=2),
+                )
 
         def quantize_weight(prod, g0, g1):
             nc.vector.quantize_mx(
@@ -316,7 +321,7 @@ def tile_picked_edgecv_gelu_p_kernel(
         round_both(7)
         look_up(1, 2, raw_tag(7, 0))
         quantize_weight(7, 0, PASSES)
-        last_fetched = sb.tile([P, V], F32, name="last_fetched")
+        last = [sb.tile([P, V], F32, name=f"last{d}") for d in range(EDGES)]
         project(4)
         look_up(2, 0)
         look_up(2, 1)
@@ -331,20 +336,21 @@ def tile_picked_edgecv_gelu_p_kernel(
         edge_features(1, 2, 0, 4, 6)
         project(7)
         edge_features(1, 0, 0, 4, 4)
-        fetch(LAST, EDGES - 1, last_fetched, 0, 2, on_scalar=True)
+        fetch(LAST, 0, last[0], 0, 2, on_scalar=True)
         edge_features(1, 1, 0, 4, 5)
+        fetch(LAST, 0, last[0], 2, 4)
+        fetch(LAST, 1, last[1], 0, 4)
+        fetch(LAST, 2, last[2], 0, 2)
+        fetch(LAST, 2, last[2], 2, 4)
         edge_features(2, 0, 0, 4, 7)
         edge_features(2, 1, 0, 4, 0)
-        look_up(3, 0)
-        look_up(3, 1)
-        fetch(LAST, EDGES - 1, last_fetched, 2, 4)
-        edge_features(2, 2, 0, 4, 1)
         larger_of_two(0, 3)
         edge_features(3, 0, 0, 4, 6)
         edge_features(3, 1, 0, 4, 4)
+        larger_of_two(3, 4)
+        edge_features(2, 2, 0, 4, 1)
         edge_features(3, 2, 0, 2, 2)
         edge_features(3, 2, 2, 4, 3)
-        larger_of_two(3, 4)
         largest(0, 4, 0, 1)
         largest(0, 4, 1, 2)
         largest(0, 4, 2, 3)

@@ -40,8 +40,16 @@ PRODUCT_BANKS = (0, 2, 0, 2, 4, 2, 0, 2)
 ROUNDED_ON_VECTOR = (3, 6, 7)
 ON_SCALAR = ((2, CENTRE), (LAST, CENTRE))
 ROUNDED_TAG = {3: "raw21", 4: "w_code1", 5: "w_code2", 6: "w_code2", 7: "w_code2"}
-ROWS_TAG = {1: "raw20", 2: "raw40", 3: "raw50"}
+ROWS_TAG = {1: "rows1", 2: "raw40", 3: "raw50"}
 SUM_BANKS = (2, 5)
+KB = 1024
+PLACES = {
+    "rows1": 0, "raw20": 2 * KB, "x_table0": 3 * KB, "raw11": 4 * KB, "raw21": 6 * KB, "raw30": 8 * KB, "raw31": 10 * KB,
+    "raw00": 12 * KB, "raw40": 12 * KB, "picked_scale": 16 * KB, "raw41": 16 * KB,
+    "scale_table": 18 * KB, "raw10": 18 * KB, "raw50": 18 * KB,
+    "raw51": 22 * KB, "x_table1": 23 * KB, "raw60": 24 * KB, "raw61": 26 * KB, "raw70": 28 * KB, "raw71": 30 * KB,
+    "w3_code": 26 * KB, "w3_scale": 30 * KB,
+}
 
 
 def tile_picked_edgecv_gelu_p_kernel(
@@ -51,7 +59,14 @@ def tile_picked_edgecv_gelu_p_kernel(
     with ExitStack() as ctx:
         lists = ctx.enter_context(tc.tile_pool(name="lists", bufs=1))
         sb = ctx.enter_context(tc.tile_pool(name="sb", bufs=1))
+        shared = ctx.enter_context(tc.tile_pool(name="shared", bufs=1))
         psum = ctx.enter_context(tc.psum_pool(name="psum", bufs=1))
+
+        def new_tile(shape, dtype, name, tag=None):
+            tag = tag or name
+            if tag in PLACES:
+                return shared.tile(shape, dtype, name=name, align_bytes=64, offset=PLACES[tag])
+            return sb.tile(shape, dtype, name=name, tag=tag, align_bytes=64)
 
         weights = {"e": w2, "y": w1}
         products = [(name, t) for t in range(TILES) for name in ("ye" if t == LAST else "ey")]
@@ -63,7 +78,7 @@ def tile_picked_edgecv_gelu_p_kernel(
             return dst
 
         def load_words(g):
-            dst = sb.tile([P, T], U32, name=f"x_table{g}", align_bytes=64)
+            dst = new_tile([P, T], U32, f"x_table{g}")
             nc.sync.dma_start(dst[:].bitcast(I32), x_words[g].rearrange("p n j -> p (n j)").bitcast(I32))
             return dst
 
@@ -74,39 +89,26 @@ def tile_picked_edgecv_gelu_p_kernel(
 
         def load_weight(prod, g):
             name, t = products[prod]
-            raw[prod, g] = sb.tile([P, PACK, P], F32, name=raw_tag(prod, g), align_bytes=64)
+            raw[prod, g] = new_tile([P, PACK, P], F32, raw_tag(prod, g))
             src = weights[name][g * P * PACK : (g + 1) * P * PACK, t * P : (t + 1) * P]
             nc.sync.dma_start(raw[prod, g][:], src.rearrange("(p j) c -> p j c", j=PACK))
 
-        scale_table = sb.tile([P, T], U8, name="scale_table", align_bytes=64)
-        nc.vector.memset(scale_table[:].bitcast(I32), 0)
-        w3_scale = sb.tile([P, N], U8, name="w3_scale", align_bytes=64)
-        nc.gpsimd.memset(w3_scale[:].bitcast(I32), 0)
+        scale_table = new_tile([P, T], U8, "scale_table")
+        nc.vector.memset(scale_table[QUADRANT : 2 * QUADRANT, :].bitcast(I32), 0)
+        nc.vector.memset(scale_table[2 * QUADRANT :, :].bitcast(I32), 0)
 
         picked = load_list(offs, "offs")
-        places = [load_list(pos1, "pos1")]
-        for q in range(P // QUADRANT):
+        rows_of_pass = SCALE_ROWS * (P // QUADRANT)
+        for g in range(PASSES):
             nc.sync.dma_start(
-                scale_table[QUADRANT * q : QUADRANT * q + SCALE_ROWS * PASSES, :].bitcast(I32),
-                x_scales[:, SCALE_ROWS * q : SCALE_ROWS * (q + 1), :].bitcast(I32),
+                scale_table[rows_of_pass * g : rows_of_pass * (g + 1), :].bitcast(I32),
+                x_scales[g].rearrange("(q r) n -> r q n", r=SCALE_ROWS).bitcast(I32),
             )
+        places = [load_list(pos1, "pos1"), load_list(pos2, "pos2"), load_list(pos3, "pos3"), load_list(cen, "cen")]
         x_table = [load_words(0)]
         load_weight(0, 0)
         x_table.append(load_words(1))
         load_weight(0, 1)
-        load_weight(1, 0)
-        load_weight(1, 1)
-        places.extend([load_list(pos2, "pos2"), load_list(pos3, "pos3"), load_list(cen, "cen")])
-        for prod in range(2, len(products)):
-            for g in range(PASSES):
-                load_weight(prod, g)
-        w3_code = sb.tile([P, 2 * N], U8, name="w3_code", align_bytes=64)
-        nc.sync.dma_start(w3_code[:].bitcast(I32), w3_words[0].bitcast(I32))
-        for q in range(P // QUADRANT):
-            nc.sync.dma_start(
-                w3_scale[QUADRANT * q : QUADRANT * q + SCALE_ROWS, :].bitcast(I32),
-                w3_scales[0, SCALE_ROWS * q : SCALE_ROWS * (q + 1), :].bitcast(I32),
-            )
 
         identity = sb.tile([P, P], F32, name="identity")
         make_identity(nc, identity[:])
@@ -117,6 +119,7 @@ def tile_picked_edgecv_gelu_p_kernel(
 
 
         x_scale = sb.tile([P, S], U8, name="x_scale", align_bytes=64)
+        nc.gpsimd.memset(x_scale[:].bitcast(I32), 0)
         x_code = [[] for g in range(PASSES)]
 
         def entries(index, lo, hi):
@@ -140,7 +143,7 @@ def tile_picked_edgecv_gelu_p_kernel(
 
         def round_weight(prod, g):
             if g == 0:
-                w_bf[prod] = sb.tile([P, PASSES, P, PACK], BF16, name=f"w_bf{prod}", tag=rounded_tag(prod), align_bytes=64)
+                w_bf[prod] = new_tile([P, PASSES, P, PACK], BF16, f"w_bf{prod}", rounded_tag(prod))
                 w_code[prod] = sb.tile([P, PASSES, P], U32, name=code_tag(prod), align_bytes=64)
                 w_scale[prod] = sb.tile([P, PASSES, P], U8, name=f"w_scale{prod}", align_bytes=64)
             if prod in ROUNDED_ON_VECTOR:
@@ -201,7 +204,7 @@ def tile_picked_edgecv_gelu_p_kernel(
         def project(prod):
             name, t = products[prod]
             tag = ROWS_TAG.get(prod, f"rows{prod}")
-            dst = sb.tile([P, S], F32, name=f"rows{prod}", tag=tag, align_bytes=64)
+            dst = new_tile([P, S], F32, f"rows{prod}", tag)
             rows[name, t] = dst
             number = PRODUCT_BANKS[prod]
             accs = [psum.tile([P, BANK], F32, name=f"acc{prod}_{h}", tag=bank(number + h)) for h in range(S // BANK)]
@@ -282,9 +285,20 @@ def tile_picked_edgecv_gelu_p_kernel(
             nc.sync.dma_start(out[:, cols], result[:])
 
 
-        nc.vector.tensor_copy(x_scale[:], scale_table[:].indirect(picked[:]))
+        picked_scale = new_tile([P, S], U8, "picked_scale")
+        nc.vector.tensor_copy(picked_scale[:], scale_table[:].indirect(picked[:]))
+        for q in range(P // QUADRANT):
+            nc.scalar.dma_start(
+                x_scale[QUADRANT * q : QUADRANT * q + SCALE_ROWS * PASSES, :].bitcast(I32),
+                picked_scale[q : QUADRANT : P // QUADRANT, :].bitcast(I32),
+            )
+        load_weight(1, 0)
         pick_words(0, 0, S, "x_code0")
+        for prod, g in ((1, 1), (2, 0), (2, 1), (3, 0), (3, 1)):
+            load_weight(prod, g)
         round_weight(0, 0)
+        load_weight(4, 0)
+        load_weight(4, 1)
         quantize_weight(0, 0, 1)
         pick_words(1, *SPANS[0], "x_code1a")
         pick_words(1, *SPANS[1], "x_code1b")
@@ -293,9 +307,11 @@ def tile_picked_edgecv_gelu_p_kernel(
         pick_words(1, *SPANS[2], raw_tag(0, 1))
         project_first()
         prepare(1)
+        for prod, g in ((5, 0), (5, 1), (6, 0), (6, 1), (7, 0), (7, 1)):
+            load_weight(prod, g)
 
         def look_up(t, d, tag=None):
-            fetch(t, d, sb.tile([P, V], F32, name=f"fetched{t}{d}", tag=tag or f"fetched{t}{d}", align_bytes=64), 0, BLOCKS)
+            fetch(t, d, new_tile([P, V], F32, f"fetched{t}{d}", tag), 0, BLOCKS)
 
         def round_both(prod):
             for g in range(PASSES):
@@ -321,6 +337,15 @@ def tile_picked_edgecv_gelu_p_kernel(
         round_both(7)
         look_up(1, 2, raw_tag(7, 0))
         quantize_weight(7, 0, PASSES)
+        w3_code = new_tile([P, 2 * N], U8, "w3_code")
+        nc.sync.dma_start(w3_code[:].bitcast(I32), w3_words[0].bitcast(I32))
+        w3_scale = new_tile([P, N], U8, "w3_scale")
+        nc.vector.memset(w3_scale[:].bitcast(I32), 0)
+        for q in range(P // QUADRANT):
+            nc.sync.dma_start(
+                w3_scale[QUADRANT * q : QUADRANT * q + SCALE_ROWS, :].bitcast(I32),
+                w3_scales[0, SCALE_ROWS * q : SCALE_ROWS * (q + 1), :].bitcast(I32),
+            )
         last = [sb.tile([P, V], F32, name=f"last{d}") for d in range(EDGES)]
         project(4)
         look_up(2, 0)

@@ -17,6 +17,8 @@ E2M1 = mybir.dt.float4_e2m1fn_x4
 GELU = mybir.ActivationFunctionType.Gelu_apprx_tanh
 COPY = mybir.ActivationFunctionType.Copy
 MAX = mybir.AluOpType.max
+MULT = mybir.AluOpType.mult
+ADD = mybir.AluOpType.add
 
 P = 128
 PACK = 4
@@ -30,26 +32,8 @@ LAST = TILES - 1
 BLOCKS = V // P
 EDGES = 3
 CENTRE = EDGES
-LOOKUPS = EDGES + 1
-
 SPANS = ((0, BANK), (BANK, BANK + BANK // 2), (BANK + BANK // 2, S))
-HALVES = ((0, BLOCKS // 2), (BLOCKS // 2, BLOCKS))
-
-PRODUCT_BANK = 0
-PRODUCT_BANKS = (0, 2, 0, 2, 4, 2, 0, 2)
-ROUNDED_ON_VECTOR = (3, 6, 7)
-ON_SCALAR = ((2, CENTRE), (LAST, CENTRE))
-ROUNDED_TAG = {3: "raw21", 4: "w_code1", 5: "w_code2", 6: "w_code2", 7: "w_code2"}
-ROWS_TAG = {1: "rows1", 2: "raw40", 3: "raw50"}
-SUM_BANKS = (2, 5)
 KB = 1024
-PLACES = {
-    "rows1": 0, "raw20": 2 * KB, "x_table0": 3 * KB, "raw11": 4 * KB, "raw21": 6 * KB, "raw30": 8 * KB, "raw31": 10 * KB,
-    "raw00": 12 * KB, "raw40": 12 * KB, "picked_scale": 16 * KB, "raw41": 16 * KB,
-    "scale_table": 18 * KB, "raw10": 18 * KB, "raw50": 18 * KB,
-    "raw51": 22 * KB, "x_table1": 23 * KB, "raw60": 24 * KB, "raw61": 26 * KB, "raw70": 28 * KB, "raw71": 30 * KB,
-    "w3_code": 26 * KB, "w3_scale": 30 * KB,
-}
 
 
 def tile_picked_edgecv_gelu_p_kernel(
@@ -62,41 +46,211 @@ def tile_picked_edgecv_gelu_p_kernel(
         shared = ctx.enter_context(tc.tile_pool(name="shared", bufs=1))
         psum = ctx.enter_context(tc.psum_pool(name="psum", bufs=1))
 
-        def new_tile(shape, dtype, name, tag=None):
-            tag = tag or name
-            if tag in PLACES:
-                return shared.tile(shape, dtype, name=name, align_bytes=64, offset=PLACES[tag])
-            return sb.tile(shape, dtype, name=name, tag=tag, align_bytes=64)
+        def new_tile(shape, dtype, name, at=None):
+            if at is None:
+                return sb.tile(shape, dtype, name=name, align_bytes=64)
+            return shared.tile(shape, dtype, name=name, align_bytes=64, offset=int(at * KB))
+
+        def bank(number):
+            return f"bank{number}"
 
         weights = {"e": w2, "y": w1}
-        products = [(name, t) for t in range(TILES) for name in ("ye" if t == LAST else "ey")]
-
 
         def load_list(src, name):
             dst = lists.tile(list(src.shape), U16, name=name)
             nc.sync.dma_start(dst[:], src)
             return dst
 
-        def load_words(g):
-            dst = new_tile([P, T], U32, f"x_table{g}")
+        def load_words(g, at=None):
+            dst = new_tile([P, T], U32, f"x_table{g}", at)
             nc.sync.dma_start(dst[:].bitcast(I32), x_words[g].rearrange("p n j -> p (n j)").bitcast(I32))
             return dst
 
-        def raw_tag(prod, g):
-            return f"raw{prod}{g}"
+        raw, w_code, w_scale, w_bf, rows, fetched = {}, {}, {}, {}, {}, {}
 
-        raw = {}
-
-        def load_weight(prod, g):
-            name, t = products[prod]
-            raw[prod, g] = new_tile([P, PACK, P], F32, raw_tag(prod, g))
+        def load_weight(prod, g, at=None):
+            name, t = prod
+            raw[prod, g] = new_tile([P, PACK, P], F32, f"raw_{name}{t}_{g}", at)
             src = weights[name][g * P * PACK : (g + 1) * P * PACK, t * P : (t + 1) * P]
             nc.sync.dma_start(raw[prod, g][:], src.rearrange("(p j) c -> p j c", j=PACK))
 
-        scale_table = new_tile([P, T], U8, "scale_table")
+        def entries(index, lo, hi):
+            return index[:, lo // PER_COLUMN : hi // PER_COLUMN]
+
+        x_code = [[] for g in range(PASSES)]
+
+        def pick_words(g, lo, hi, at=None):
+            dst = new_tile([P, hi - lo], U32, f"x_code{g}_{lo}", at)
+            nc.vector.tensor_copy(dst[:], x_table[g][:].indirect(entries(picked, lo, hi)))
+            x_code[g].append((lo, hi, dst))
+
+        def round_weight(prod, g, engine, at=None):
+            name, t = prod
+            w_bf[prod, g] = new_tile([P, P, PACK], BF16, f"w_bf_{name}{t}_{g}", at)
+            if engine == "scalar":
+                nc.scalar.copy(
+                    w_bf[prod, g][:].rearrange("p (c i) j -> p c j i", i=PACK),
+                    raw[prod, g][:].rearrange("p j (c i) -> p c j i", i=PACK),
+                )
+            elif engine == "vector":
+                nc.vector.tensor_copy(w_bf[prod, g][:], raw[prod, g][:].rearrange("p j c -> p c j"))
+            else:
+                nc.gpsimd.tensor_scalar(w_bf[prod, g][:], raw[prod, g][:].rearrange("p j c -> p c j"), 1.0, 0.0, MULT, ADD)
+
+        def round_product(prod, at):
+            name, t = prod
+            both = new_tile([P, PASSES, P, PACK], BF16, f"w_bf_{name}{t}", at)
+            w_bf[prod] = both
+            nc.gpsimd.tensor_scalar(both[:], raw[prod][:].rearrange("p g j c -> p g c j"), 1.0, 0.0, MULT, ADD)
+
+        def round_half(prod, g, at=None):
+            name, t = prod
+            if g == 0:
+                w_bf[prod] = new_tile([P, PASSES, P, PACK], BF16, f"w_bf_{name}{t}", at)
+            nc.scalar.copy(
+                w_bf[prod][:, g].rearrange("p (c i) j -> p c j i", i=PACK),
+                raw[prod, g][:].rearrange("p j (c i) -> p c j i", i=PACK),
+            )
+
+        def load_product(prod, at=None):
+            name, t = prod
+            raw[prod] = new_tile([P, PASSES, PACK, P], F32, f"raw_{name}{t}", at)
+            for g in range(PASSES):
+                src = weights[name][g * P * PACK : (g + 1) * P * PACK, t * P : (t + 1) * P]
+                nc.sync.dma_start(raw[prod][:, g], src.rearrange("(p j) c -> p j c", j=PACK))
+
+        def quantize_product(prod, at=None):
+            name, t = prod
+            code = new_tile([P, PASSES, P], U32, f"w_code_{name}{t}", at)
+            scale = new_tile([P, PASSES, P], U8, f"w_scale_{name}{t}")
+            for g in range(PASSES):
+                w_code[prod, g], w_scale[prod, g] = code[:, g], scale[:, g]
+            nc.vector.quantize_mx(
+                out=code[:].rearrange("p g c -> p (g c)").bitcast(E4M3),
+                scales=scale[:].rearrange("p g c -> p (g c)"),
+                in_=w_bf[prod][:].rearrange("p g c j -> p (g c j)"),
+            )
+
+        def quantize_weight(prod, g, at=None):
+            name, t = prod
+            w_code[prod, g] = new_tile([P, P], U32, f"w_code_{name}{t}_{g}", at)[:]
+            w_scale[prod, g] = new_tile([P, P], U8, f"w_scale_{name}{t}_{g}")[:]
+            nc.vector.quantize_mx(
+                out=w_code[prod, g].bitcast(E4M3),
+                scales=w_scale[prod, g],
+                in_=w_bf[prod, g][:].rearrange("p c j -> p (c j)"),
+            )
+
+        accs = {}
+
+        def multiply(prod, g, lo, hi, number):
+            name, t = prod
+            if g == 0:
+                accs[prod, lo] = psum.tile([P, hi - lo], F32, name=f"acc_{name}{t}_{lo}", tag=bank(number))
+            acc = accs[prod, lo]
+            for first, end, words in x_code[g]:
+                c0, c1 = max(lo, first), min(hi, end)
+                if c0 < c1:
+                    nc.tensor.matmul_mx(
+                        out=acc[:, c0 - lo : c1 - lo],
+                        lhsT=w_code[prod, g].bitcast(E4M3),
+                        lhsT_scale=w_scale[prod, g],
+                        rhs=words[:, c0 - first : c1 - first].bitcast(E4M3),
+                        rhs_scale=x_scale[SCALE_ROWS * g :, c0:c1],
+                        start=(g == 0),
+                        stop=(g == PASSES - 1 and c1 == hi),
+                    )
+
+        def product(prod, number):
+            for h in range(S // BANK):
+                for g in range(PASSES):
+                    multiply(prod, g, h * BANK, (h + 1) * BANK, number + h)
+
+        def empty(prod, lo, hi, engine="scalar", at=None):
+            name, t = prod
+            if prod not in rows:
+                rows[prod] = new_tile([P, S], F32, f"rows_{name}{t}", at)
+            copy = nc.scalar.copy if engine == "scalar" else nc.vector.tensor_copy
+            copy(rows[prod][:, lo:hi], accs[prod, lo][:])
+
+        def empty_both(prod, at=None):
+            for h in range(S // BANK):
+                empty(prod, h * BANK, (h + 1) * BANK, "scalar", at)
+
+        def look_up(t, d, engine="vector", at=None, b0=0, b1=BLOCKS):
+            dst = new_tile([P, (b1 - b0) * P], F32, f"fetched{t}{d}{b0}", at)
+            for b in range(b0, b1):
+                fetched[t, d, b] = dst[:, (b - b0) * P : (b - b0 + 1) * P]
+            source = rows["y" if d == CENTRE else "e", t]
+            looked_up = source[:].indirect(entries(places[d], b0 * P, b1 * P))
+            if engine == "scalar":
+                nc.scalar.activation(dst[:], looked_up, COPY)
+            else:
+                nc.vector.tensor_copy(dst[:], looked_up)
+
+        feats = sb.tile([P, EDGES, BLOCKS, TILES, P], BF16, name="feats")
+        pair = sb.tile([P, BLOCKS, TILES, P], BF16, name="pair")
+        z_row = sb.tile([P, BLOCKS, TILES, P], BF16, name="z_row")
+        sums = {}
+
+        def turn(t, d, number, opens, b0=0, b1=BLOCKS):
+            sums[t, d, b0] = psum.tile([P, b1 - b0, P], F32, name=f"sums{t}{d}{b0}", tag=bank(number))
+            adds = d if opens == CENTRE else CENTRE
+            for b in range(b0, b1):
+                nc.tensor.matmul(sums[t, d, b0][:, b - b0], fetched[t, opens, b], identity[:], start=(b == b0), stop=False, is_transpose=True)
+            for b in range(b0, b1):
+                nc.tensor.matmul(sums[t, d, b0][:, b - b0], fetched[t, adds, b], identity[:], start=False, stop=(b == b1 - 1), is_transpose=True)
+
+        def gelu(t, d, b0=0, b1=BLOCKS):
+            nc.scalar.activation(feats[:, d, b0:b1, t], sums[t, d, b0][:], GELU, bias=no_bias[:])
+
+        def features(t, d, number, opens, b0=0, b1=BLOCKS):
+            turn(t, d, number, opens, b0, b1)
+            gelu(t, d, b0, b1)
+
+        def larger_of_two(t0, t1, b0=0, b1=BLOCKS):
+            nc.vector.tensor_tensor(pair[:, b0:b1, t0:t1], feats[:, 0, b0:b1, t0:t1], feats[:, 1, b0:b1, t0:t1], MAX)
+
+        def largest(b0, b1, t0=0, t1=TILES):
+            nc.vector.tensor_tensor(z_row[:, b0:b1, t0:t1], pair[:, b0:b1, t0:t1], feats[:, 2, b0:b1, t0:t1], MAX)
+
+        z_bf, z_code, z_scale, result = {}, {}, {}, {}
+
+        def turn_back(b, number, engine="scalar"):
+            words = z_row[:, b].rearrange("p t c -> p (t c)").bitcast(F32)
+            turned = psum.tile([P, 2, P], F32, name=f"turned{b}", tag=bank(number))
+            for u in range(2):
+                nc.tensor.transpose(turned[:, u], words[:, u::2], identity[:])
+            z_bf[b] = new_tile([P, P, PACK], BF16, f"z_bf{b}")
+            copy = nc.scalar.copy if engine == "scalar" else nc.vector.tensor_copy
+            copy(z_bf[b][:].bitcast(F32), turned[:].rearrange("p u v -> p v u"))
+
+        def project(b, number, engine="scalar"):
+            z_code[b] = new_tile([P, P], U32, f"z_code{b}")
+            z_scale[b] = new_tile([P, P], U8, f"z_scale{b}")
+            nc.vector.quantize_mx(out=z_code[b][:].bitcast(E4M3), scales=z_scale[b][:], in_=z_bf[b][:].rearrange("p v j -> p (v j)"))
+            acc = psum.tile([P, P], F32, name=f"out{b}", tag=bank(number))
+            nc.tensor.matmul_mx(
+                out=acc[:],
+                lhsT=w3_code[:].bitcast(E2M1),
+                lhsT_scale=w3_scale[:],
+                rhs=z_code[b][:].bitcast(E4M3),
+                rhs_scale=z_scale[b][:],
+                start=True,
+                stop=True,
+            )
+            result[b] = new_tile([P, P], F32, f"result{b}")
+            copy = nc.scalar.copy if engine == "scalar" else nc.vector.tensor_copy
+            copy(result[b][:], acc[:])
+            nc.sync.dma_start(out[:, b * P : (b + 1) * P], result[b][:])
+
+        e0, e1, e2, e3 = (("e", t) for t in range(TILES))
+        y0, y1, y2, y3 = (("y", t) for t in range(TILES))
+
+
+        scale_table = new_tile([P, T], U8, "scale_table", 4)
         nc.vector.memset(scale_table[QUADRANT : 2 * QUADRANT, :].bitcast(I32), 0)
         nc.vector.memset(scale_table[2 * QUADRANT :, :].bitcast(I32), 0)
-
         picked = load_list(offs, "offs")
         rows_of_pass = SCALE_ROWS * (P // QUADRANT)
         for g in range(PASSES):
@@ -105,186 +259,18 @@ def tile_picked_edgecv_gelu_p_kernel(
                 x_scales[g].rearrange("(q r) n -> r q n", r=SCALE_ROWS).bitcast(I32),
             )
         places = [load_list(pos1, "pos1"), load_list(pos2, "pos2"), load_list(pos3, "pos3"), load_list(cen, "cen")]
-        x_table = [load_words(0)]
-        load_weight(0, 0)
-        x_table.append(load_words(1))
-        load_weight(0, 1)
-
+        x_table = [load_words(0, 15)]
+        load_weight(e0, 0)
+        x_table.append(load_words(1, 26))
+        load_weight(e0, 1, 42)
         identity = sb.tile([P, P], F32, name="identity")
         make_identity(nc, identity[:])
         zero = sb.tile([P, 1], F32, name="zero")
         nc.vector.memset(zero[:], 0.0)
         no_bias = sb.tile([P, 1], F32, name="no_bias")
         nc.scalar.activation(no_bias[:], zero[:], GELU)
-
-
-        x_scale = sb.tile([P, S], U8, name="x_scale", align_bytes=64)
+        x_scale = new_tile([P, S], U8, "x_scale")
         nc.gpsimd.memset(x_scale[:].bitcast(I32), 0)
-        x_code = [[] for g in range(PASSES)]
-
-        def entries(index, lo, hi):
-            return index[:, lo // PER_COLUMN : hi // PER_COLUMN]
-
-        def pick_words(g, lo, hi, tag):
-            dst = sb.tile([P, hi - lo], U32, name=f"x_code{g}_{lo}", tag=tag, align_bytes=64)
-            nc.vector.tensor_copy(dst[:], x_table[g][:].indirect(entries(picked, lo, hi)))
-            x_code[g].append((lo, hi, dst))
-
-
-        w_code, w_scale, w_bf = {}, {}, {}
-
-        def code_tag(prod):
-            return f"w_code{prod}"
-
-        def rounded_tag(prod):
-            if prod in ROUNDED_TAG:
-                return ROUNDED_TAG[prod]
-            return code_tag(prod - 2) if prod >= 2 else f"w_bf{prod}"
-
-        def round_weight(prod, g):
-            if g == 0:
-                w_bf[prod] = new_tile([P, PASSES, P, PACK], BF16, f"w_bf{prod}", rounded_tag(prod))
-                w_code[prod] = sb.tile([P, PASSES, P], U32, name=code_tag(prod), align_bytes=64)
-                w_scale[prod] = sb.tile([P, PASSES, P], U8, name=f"w_scale{prod}", align_bytes=64)
-            if prod in ROUNDED_ON_VECTOR:
-                nc.vector.tensor_copy(
-                    w_bf[prod][:, g].rearrange("p (u m o) j -> p m u o j", u=2, o=2),
-                    raw[prod, g][:].rearrange("p j (m u o) -> p m u o j", u=2, o=2),
-                )
-            else:
-                nc.scalar.copy(
-                    w_bf[prod][:, g].rearrange("p (u m o) j -> p m j u o", u=2, o=2),
-                    raw[prod, g][:].rearrange("p j (m u o) -> p m j u o", u=2, o=2),
-                )
-
-        def quantize_weight(prod, g0, g1):
-            nc.vector.quantize_mx(
-                out=w_code[prod][:, g0:g1].rearrange("p g c -> p (g c)").bitcast(E4M3),
-                scales=w_scale[prod][:, g0:g1].rearrange("p g c -> p (g c)"),
-                in_=w_bf[prod][:, g0:g1].rearrange("p g c j -> p (g c j)"),
-            )
-
-        def prepare(prod):
-            for g in range(PASSES):
-                round_weight(prod, g)
-            quantize_weight(prod, 0, PASSES)
-
-
-        rows = {}
-
-        def bank(number):
-            return f"bank{number}"
-
-        def multiply(prod, g, lo, hi, acc):
-            for first, end, words in x_code[g]:
-                c0, c1 = max(lo, first), min(hi, end)
-                if c0 < c1:
-                    nc.tensor.matmul_mx(
-                        out=acc[:, c0 - lo : c1 - lo],
-                        lhsT=w_code[prod][:, g].bitcast(E4M3),
-                        lhsT_scale=w_scale[prod][:, g],
-                        rhs=words[:, c0 - first : c1 - first].bitcast(E4M3),
-                        rhs_scale=x_scale[SCALE_ROWS * g :, c0:c1],
-                        start=(g == 0),
-                        stop=(g == PASSES - 1 and c1 == hi),
-                    )
-
-        def project_first():
-            dst = sb.tile([P, S], F32, name="rows0", align_bytes=64)
-            rows[products[0]] = dst
-            numbers = (PRODUCT_BANK, PRODUCT_BANK + 1, SUM_BANKS[0] + 2)
-            accs = [psum.tile([P, hi - lo], F32, name=f"acc0_{lo}", tag=bank(number)) for number, (lo, hi) in zip(numbers, SPANS)]
-            for g in range(PASSES):
-                for acc, (lo, hi) in zip(accs, SPANS):
-                    multiply(0, g, lo, hi, acc)
-            for acc, (lo, hi) in zip(accs, SPANS):
-                copy = nc.vector.tensor_copy if lo == 0 else nc.scalar.copy
-                copy(dst[:, lo:hi], acc[:])
-
-        def project(prod):
-            name, t = products[prod]
-            tag = ROWS_TAG.get(prod, f"rows{prod}")
-            dst = new_tile([P, S], F32, f"rows{prod}", tag)
-            rows[name, t] = dst
-            number = PRODUCT_BANKS[prod]
-            accs = [psum.tile([P, BANK], F32, name=f"acc{prod}_{h}", tag=bank(number + h)) for h in range(S // BANK)]
-            for h, acc in enumerate(accs):
-                for g in range(PASSES):
-                    multiply(prod, g, h * BANK, (h + 1) * BANK, acc)
-            for h, acc in enumerate(accs):
-                nc.scalar.copy(dst[:, h * BANK : (h + 1) * BANK], acc[:])
-
-
-        fetched = {}
-
-        def lookup_order(t):
-            return (CENTRE, 0, 1, 2) if t == LAST else (0, 1, CENTRE, 2)
-
-        def fetch(t, d, dst, b0, b1, on_scalar=False):
-            fetched[t, d] = dst
-            source = rows["y" if d == CENTRE else "e", t]
-            looked_up = source[:].indirect(entries(places[d], b0 * P, b1 * P))
-            if on_scalar or (t, d) in ON_SCALAR:
-                nc.scalar.activation(dst[:, b0 * P : b1 * P], looked_up, COPY)
-            else:
-                nc.vector.tensor_copy(dst[:, b0 * P : b1 * P], looked_up)
-
-        feats = sb.tile([P, TILES, EDGES, V], BF16, name="feats")
-
-        def edge_features(t, d, b0, b1, number):
-            sums = psum.tile([P, b1 - b0, P], F32, name=f"sums{t}{d}{b0}", tag=bank(number))
-            opens, adds = sorted((d, CENTRE), key=lambda look_up: lookup_order(t).index(look_up))
-            for b in range(b0, b1):
-                block = fetched[t, opens][:, b * P : (b + 1) * P]
-                nc.tensor.matmul(sums[:, b - b0], block, identity[:], start=(b == b0), stop=False, is_transpose=True)
-            for b in range(b0, b1):
-                block = fetched[t, adds][:, b * P : (b + 1) * P]
-                nc.tensor.matmul(sums[:, b - b0], block, identity[:], start=False, stop=(b == b1 - 1), is_transpose=True)
-            nc.scalar.activation(feats[:, t, d, b0 * P : b1 * P], sums[:].rearrange("p b c -> p (b c)"), GELU, bias=no_bias[:])
-
-
-        z_row = sb.tile([P, BLOCKS * H], BF16, name="z_row")
-        z_runs = z_row[:].rearrange("p (r t c) -> p t r c", t=TILES, c=P // 2)
-        pair = sb.tile([P, TILES, V], BF16, name="pair")
-
-        def larger_of_two(t0, t1):
-            nc.vector.tensor_tensor(pair[:, t0:t1], feats[:, t0:t1, 0], feats[:, t0:t1, 1], MAX)
-
-        def largest(t0, t1, b0, b1):
-            cols = slice(b0 * P, b1 * P)
-            nc.vector.tensor_tensor(
-                z_runs[:, t0:t1, 2 * b0 : 2 * b1],
-                pair[:, t0:t1, cols].rearrange("p t (r c) -> p t r c", c=P // 2),
-                feats[:, t0:t1, 2, cols].rearrange("p t (r c) -> p t r c", c=P // 2),
-                MAX,
-            )
-
-        def finish(b, turned_bank, out_bank, copy=nc.scalar.copy):
-            cols = slice(b * P, (b + 1) * P)
-            words = z_row[:, b * H : (b + 1) * H].bitcast(F32)
-            turned = psum.tile([P, 2, P], F32, name=f"turned{b}", tag=bank(turned_bank))
-            for u in range(2):
-                nc.tensor.transpose(turned[:, u], words[:, u * P : (u + 1) * P], identity[:])
-            z_bf = sb.tile([P, P, PACK], BF16, name=f"z_bf{b}", align_bytes=64)
-            copy(z_bf[:].bitcast(F32), turned[:].rearrange("p u v -> p v u"))
-            z_code = sb.tile([P, P], U32, name=f"z_code{b}", align_bytes=64)
-            z_scale = sb.tile([P, P], U8, name=f"z_scale{b}", align_bytes=64)
-            nc.vector.quantize_mx(out=z_code[:].bitcast(E4M3), scales=z_scale[:], in_=z_bf[:].rearrange("p v j -> p (v j)"))
-            acc = psum.tile([P, P], F32, name=f"out{b}", tag=bank(out_bank))
-            nc.tensor.matmul_mx(
-                out=acc[:],
-                lhsT=w3_code[:].bitcast(E2M1),
-                lhsT_scale=w3_scale[:],
-                rhs=z_code[:].bitcast(E4M3),
-                rhs_scale=z_scale[:],
-                start=True,
-                stop=True,
-            )
-            result = sb.tile([P, P], F32, name=f"result{b}")
-            nc.scalar.copy(result[:], acc[:])
-            nc.sync.dma_start(out[:, cols], result[:])
-
-
         picked_scale = new_tile([P, S], U8, "picked_scale")
         nc.vector.tensor_copy(picked_scale[:], scale_table[:].indirect(picked[:]))
         for q in range(P // QUADRANT):
@@ -292,95 +278,124 @@ def tile_picked_edgecv_gelu_p_kernel(
                 x_scale[QUADRANT * q : QUADRANT * q + SCALE_ROWS * PASSES, :].bitcast(I32),
                 picked_scale[q : QUADRANT : P // QUADRANT, :].bitcast(I32),
             )
-        load_weight(1, 0)
-        pick_words(0, 0, S, "x_code0")
-        for prod, g in ((1, 1), (2, 0), (2, 1), (3, 0), (3, 1)):
-            load_weight(prod, g)
-        round_weight(0, 0)
-        load_weight(4, 0)
-        load_weight(4, 1)
-        quantize_weight(0, 0, 1)
-        pick_words(1, *SPANS[0], "x_code1a")
-        pick_words(1, *SPANS[1], "x_code1b")
-        round_weight(0, 1)
-        quantize_weight(0, 1, 2)
-        pick_words(1, *SPANS[2], raw_tag(0, 1))
-        project_first()
-        prepare(1)
-        for prod, g in ((5, 0), (5, 1), (6, 0), (6, 1), (7, 0), (7, 1)):
-            load_weight(prod, g)
-
-        def look_up(t, d, tag=None):
-            fetch(t, d, new_tile([P, V], F32, f"fetched{t}{d}", tag), 0, BLOCKS)
-
-        def round_both(prod):
-            for g in range(PASSES):
-                round_weight(prod, g)
-
-        look_up(0, 0)
-        prepare(2)
-        project(1)
-        round_both(3)
-        look_up(0, 1, rounded_tag(2))
-        quantize_weight(3, 0, PASSES)
-        look_up(0, 2, raw_tag(3, 1))
-        prepare(4)
-        look_up(0, CENTRE, raw_tag(4, 1))
-        project(2)
-        prepare(5)
-        look_up(1, 0, raw_tag(5, 1))
-        project(3)
-        round_both(6)
-        look_up(1, 1, raw_tag(6, 0))
-        quantize_weight(6, 0, PASSES)
-        look_up(1, CENTRE)
-        round_both(7)
-        look_up(1, 2, raw_tag(7, 0))
-        quantize_weight(7, 0, PASSES)
-        w3_code = new_tile([P, 2 * N], U8, "w3_code")
+        load_weight(y0, 0, 5)
+        load_weight(y0, 1, 3)
+        pick_words(0, 0, S)
+        load_product(e1, 12)
+        load_weight(y1, 0, 16)
+        load_weight(y1, 1, 21)
+        round_weight(e0, 0, "scalar")
+        quantize_weight(e0, 0)
+        for n, (lo, hi) in enumerate(SPANS):
+            multiply(e0, 0, lo, hi, n)
+        pick_words(1, *SPANS[0])
+        round_weight(e0, 1, "scalar")
+        pick_words(1, *SPANS[1])
+        quantize_weight(e0, 1, 36)
+        pick_words(1, *SPANS[2], 42)
+        load_product(e2, 26)
+        load_product(y2, 31)
+        for n, (lo, hi) in enumerate(SPANS):
+            multiply(e0, 1, lo, hi, n)
+        round_half(y0, 0, 19)
+        round_half(y0, 1)
+        load_product(y3, 6)
+        load_product(e3, 0)
+        w3_code = new_tile([P, 2 * N], U8, "w3_code", 30)
         nc.sync.dma_start(w3_code[:].bitcast(I32), w3_words[0].bitcast(I32))
-        w3_scale = new_tile([P, N], U8, "w3_scale")
+        w3_scale = new_tile([P, N], U8, "w3_scale", 30.5)
         nc.vector.memset(w3_scale[:].bitcast(I32), 0)
         for q in range(P // QUADRANT):
             nc.sync.dma_start(
                 w3_scale[QUADRANT * q : QUADRANT * q + SCALE_ROWS, :].bitcast(I32),
                 w3_scales[0, SCALE_ROWS * q : SCALE_ROWS * (q + 1), :].bitcast(I32),
             )
-        last = [sb.tile([P, V], F32, name=f"last{d}") for d in range(EDGES)]
-        project(4)
-        look_up(2, 0)
-        look_up(2, 1)
-        look_up(2, 2)
-        project(5)
-        edge_features(0, 0, 0, 4, 6)
-        look_up(2, CENTRE)
-        edge_features(0, 1, 0, 4, 4)
-        project(6)
-        edge_features(0, 2, 0, 4, 5)
-        look_up(3, CENTRE)
-        edge_features(1, 2, 0, 4, 6)
-        project(7)
-        edge_features(1, 0, 0, 4, 4)
-        fetch(LAST, 0, last[0], 0, 2, on_scalar=True)
-        edge_features(1, 1, 0, 4, 5)
-        fetch(LAST, 0, last[0], 2, 4)
-        fetch(LAST, 1, last[1], 0, 4)
-        fetch(LAST, 2, last[2], 0, 2)
-        fetch(LAST, 2, last[2], 2, 4)
-        edge_features(2, 0, 0, 4, 7)
-        edge_features(2, 1, 0, 4, 0)
-        larger_of_two(0, 3)
-        edge_features(3, 0, 0, 4, 6)
-        edge_features(3, 1, 0, 4, 4)
-        larger_of_two(3, 4)
-        edge_features(2, 2, 0, 4, 1)
-        edge_features(3, 2, 0, 2, 2)
-        edge_features(3, 2, 2, 4, 3)
-        largest(0, 4, 0, 1)
-        largest(0, 4, 1, 2)
-        largest(0, 4, 2, 3)
-        largest(0, 4, 3, 4)
-        finish(0, 5, 6)
-        finish(1, 7, 4)
-        finish(2, 0, 2)
-        finish(3, 1, 3)
+        quantize_product(y0)
+        empty(e0, *SPANS[0], "vector")
+        empty(e0, *SPANS[1])
+        empty(e0, *SPANS[2])
+        product(y0, 3)
+        round_product(e1, 19)
+        round_half(y1, 0, 36)
+        round_half(y1, 1)
+        look_up(0, 0, "vector")
+        quantize_product(e1, 17)
+        quantize_product(y1)
+        round_product(e2, 37)
+        product(e1, 0)
+        product(y1, 5)
+        empty_both(y0, 22)
+        look_up(0, 1, "vector", 20)
+        look_up(0, 2, "vector", 35)
+        empty_both(e1)
+        look_up(0, CENTRE, "scalar", 17)
+        quantize_product(e2)
+        round_product(y2, 38)
+        product(e2, 0)
+        look_up(1, 0, "vector", 26)
+        look_up(1, 1, "vector", 28)
+        empty_both(y1)
+        turn(0, 0, 5, 0)
+        turn(0, 1, 6, 1)
+        empty_both(e2)
+        quantize_product(y2)
+        round_product(y3, 39)
+        product(y2, 3)
+        look_up(1, 2, "vector", 31)
+        look_up(1, CENTRE, "vector", 33)
+        gelu(0, 0)
+        gelu(0, 1)
+        turn(0, 2, 0, 2)
+        quantize_product(y3)
+        round_product(e3, 40)
+        empty_both(y2)
+        gelu(0, 2)
+        turn(1, 0, 5, 0)
+        product(y3, 1)
+        look_up(2, 0, "vector", 6)
+        look_up(2, 1, "vector", 8)
+        look_up(2, CENTRE, "scalar")
+        turn(1, 1, 0, 1)
+        empty_both(y3)
+        quantize_product(e3)
+        turn(2, 0, 6, 0)
+        product(e3, 3)
+        gelu(1, 0)
+        gelu(1, 1)
+        turn(1, 2, 5, 2)
+        look_up(2, 2, "vector", 0)
+        look_up(3, CENTRE, "vector", 2)
+        larger_of_two(0, 2)
+        turn(2, 1, 0, 1)
+        empty_both(e3)
+        turn(2, 2, 3, 2)
+        gelu(1, 2)
+        gelu(2, 0)
+        gelu(2, 1)
+        gelu(2, 2)
+        look_up(3, 0, "vector", None, 0, 2)
+        features(3, 0, 4, CENTRE, 0, 2)
+        look_up(3, 1, "vector", None, 0, 2)
+        features(3, 1, 5, CENTRE, 0, 2)
+        look_up(3, 2, "vector", None, 0, 2)
+        features(3, 2, 6, CENTRE, 0, 2)
+        look_up(3, 0, "vector", None, 2, 4)
+        features(3, 0, 0, CENTRE, 2, 4)
+        look_up(3, 1, "vector", None, 2, 4)
+        features(3, 1, 3, CENTRE, 2, 4)
+        look_up(3, 2, "vector", None, 2, 4)
+        features(3, 2, 4, CENTRE, 2, 4)
+        larger_of_two(2, 4, 0, 2)
+        largest(0, 1)
+        largest(1, 2)
+        larger_of_two(2, 4, 2, 4)
+        turn_back(0, 1)
+        turn_back(1, 2)
+        largest(2, 3)
+        largest(3, 4)
+        project(0, 5)
+        project(1, 6)
+        turn_back(2, 7)
+        turn_back(3, 0)
+        project(2, 3)
+        project(3, 4)

@@ -156,7 +156,7 @@ def tile_picked_edgecv_gelu_p_kernel(
                         lhsT=w_code[prod, g].bitcast(E4M3),
                         lhsT_scale=w_scale[prod, g],
                         rhs=words[:, c0 - first : c1 - first].bitcast(E4M3),
-                        rhs_scale=x_scale[SCALE_ROWS * g :, c0:c1],
+                        rhs_scale=x_scale[:, g * S + c0 : g * S + c1],
                         start=(g == 0),
                         stop=(g == PASSES - 1 and c1 == hi),
                     )
@@ -177,10 +177,21 @@ def tile_picked_edgecv_gelu_p_kernel(
             for h in range(S // BANK):
                 empty(prod, h * BANK, (h + 1) * BANK, "scalar", at)
 
+        def look_up_sum(t, d, at=None, b0=0, b1=BLOCKS):
+            dst = new_tile([P, (b1 - b0) * P], F32, f"summed{t}{d}{b0}", at)
+            for b in range(b0, b1):
+                fetched[t, d, b] = dst[:, (b - b0) * P : (b - b0 + 1) * P]
+            looked_up = rows["e", t][:].indirect(entries(places[d], b0 * P, b1 * P))
+            nc.vector.tensor_tensor(dst[:], looked_up, centres[t][:, b0 * P : b1 * P], ADD)
+
+        centres = {}
+
         def look_up(t, d, engine="vector", at=None, b0=0, b1=BLOCKS):
             dst = new_tile([P, (b1 - b0) * P], F32, f"fetched{t}{d}{b0}", at)
             for b in range(b0, b1):
                 fetched[t, d, b] = dst[:, (b - b0) * P : (b - b0 + 1) * P]
+            if d == CENTRE:
+                centres[t] = dst
             source = rows["y" if d == CENTRE else "e", t]
             looked_up = source[:].indirect(entries(places[d], b0 * P, b1 * P))
             if engine == "scalar":
@@ -188,39 +199,83 @@ def tile_picked_edgecv_gelu_p_kernel(
             else:
                 nc.vector.tensor_copy(dst[:], looked_up)
 
-        feats = sb.tile([P, EDGES, BLOCKS, TILES, P], BF16, name="feats")
-        pair = sb.tile([P, BLOCKS, TILES, P], BF16, name="pair")
-        z_row = sb.tile([P, BLOCKS, TILES, P], BF16, name="z_row")
+        feats = {}
+        third = sb.tile([P, BLOCKS, 2, TILES, P // 2], BF16, name="third")
+        pairs = []
+        z_row = sb.tile([P, BLOCKS, 2, TILES, P // 2], BF16, name="z_row")
         sums = {}
 
         def turn(t, d, number, opens, b0=0, b1=BLOCKS):
             sums[t, d, b0] = psum.tile([P, b1 - b0, P], F32, name=f"sums{t}{d}{b0}", tag=bank(number))
+            if opens is None:
+                for b in range(b0, b1):
+                    nc.tensor.transpose(sums[t, d, b0][:, b - b0], fetched[t, d, b], identity[:])
+                return
             adds = d if opens == CENTRE else CENTRE
             for b in range(b0, b1):
                 nc.tensor.matmul(sums[t, d, b0][:, b - b0], fetched[t, opens, b], identity[:], start=(b == b0), stop=False, is_transpose=True)
             for b in range(b0, b1):
                 nc.tensor.matmul(sums[t, d, b0][:, b - b0], fetched[t, adds, b], identity[:], start=False, stop=(b == b1 - 1), is_transpose=True)
 
-        def gelu(t, d, b0=0, b1=BLOCKS):
-            nc.scalar.activation(feats[:, d, b0:b1, t], sums[t, d, b0][:], GELU, bias=no_bias[:])
+        def gelu(t, d, b0=0, b1=BLOCKS, at=None):
+            if d == EDGES - 1:
+                dst = third[:, b0:b1, :, t].rearrange("p b u (m o) -> p u b m o", o=2)
+            else:
+                if (t, d) not in feats:
+                    feats[t, d] = new_tile([P, 2, BLOCKS, P // 2], BF16, f"feats{t}{d}", at)
+                dst = feats[t, d][:, :, b0:b1].rearrange("p u b (m o) -> p u b m o", o=2)
+            nc.scalar.activation(
+                dst,
+                sums[t, d, b0][:].rearrange("p b (m u o) -> p u b m o", u=2, o=2),
+                GELU,
+                bias=no_bias[:],
+            )
 
         def features(t, d, number, opens, b0=0, b1=BLOCKS):
             turn(t, d, number, opens, b0, b1)
             gelu(t, d, b0, b1)
 
-        def larger_of_two(t0, t1, b0=0, b1=BLOCKS):
-            nc.vector.tensor_tensor(pair[:, b0:b1, t0:t1], feats[:, 0, b0:b1, t0:t1], feats[:, 1, b0:b1, t0:t1], MAX)
+        def larger_of_two(t, b0=0, b1=BLOCKS, at=None):
+            if not pairs:
+                pairs.append(new_tile([P, BLOCKS, 2, TILES, P // 2], BF16, "pair", at))
+            dst = pairs[0][:, b0:b1, :, t].rearrange("p b u c -> p u b c")
+            nc.vector.tensor_tensor(dst, feats[t, 0][:, :, b0:b1], feats[t, 1][:, :, b0:b1], MAX)
 
-        def largest(b0, b1, t0=0, t1=TILES):
-            nc.vector.tensor_tensor(z_row[:, b0:b1, t0:t1], pair[:, b0:b1, t0:t1], feats[:, 2, b0:b1, t0:t1], MAX)
+        def largest(b):
+            nc.vector.tensor_tensor(z_row[:, b], pairs[0][:, b], third[:, b], MAX)
+
+        def turn_words(src, b, number, name):
+            words = src[:, b].rearrange("p u t c -> p (u t c)").bitcast(F32)
+            turned = psum.tile([P, 2, P], F32, name=f"{name}{b}", tag=bank(number))
+            for u in range(2):
+                nc.tensor.transpose(turned[:, u], words[:, u * P : (u + 1) * P], identity[:])
+            return turned
+
+        pair_turned = {}
+
+        def turn_pair(b, number, engine="scalar"):
+            turned = turn_words(pairs[0], b, number, "pair_words")
+            pair_turned[b] = new_tile([P, P, PACK], BF16, f"pair_turned{b}")
+            copy = nc.scalar.copy if engine == "scalar" else nc.vector.tensor_copy
+            copy(pair_turned[b][:].bitcast(F32), turned[:].rearrange("p u v -> p v u"))
+
+        def largest_turned(b, number):
+            turned = turn_words(third, b, number, "third_words")
+            z_bf[b] = new_tile([P, P, PACK], BF16, f"z_bf{b}")
+            nc.vector.tensor_tensor(
+                z_bf[b][:].rearrange("p v (u o) -> p v u o", o=2),
+                turned[:].bitcast(BF16).rearrange("p u (v o) -> p v u o", o=2),
+                pair_turned[b][:].rearrange("p v (u o) -> p v u o", o=2),
+                MAX,
+            )
 
         z_bf, z_code, z_scale, result = {}, {}, {}, {}
 
         def turn_back(b, number, engine="scalar"):
-            words = z_row[:, b].rearrange("p t c -> p (t c)").bitcast(F32)
+            words = z_row[:, b].rearrange("p u t c -> p (u t c)").bitcast(F32)
             turned = psum.tile([P, 2, P], F32, name=f"turned{b}", tag=bank(number))
             for u in range(2):
-                nc.tensor.transpose(turned[:, u], words[:, u::2], identity[:])
+                nc.tensor.transpose(turned[:, u], words[:, u * P : (u + 1) * P], identity[:])
             z_bf[b] = new_tile([P, P, PACK], BF16, f"z_bf{b}")
             copy = nc.scalar.copy if engine == "scalar" else nc.vector.tensor_copy
             copy(z_bf[b][:].bitcast(F32), turned[:].rearrange("p u v -> p v u"))
@@ -252,12 +307,10 @@ def tile_picked_edgecv_gelu_p_kernel(
         nc.vector.memset(scale_table[QUADRANT : 2 * QUADRANT, :].bitcast(I32), 0)
         nc.vector.memset(scale_table[2 * QUADRANT :, :].bitcast(I32), 0)
         picked = load_list(offs, "offs")
-        rows_of_pass = SCALE_ROWS * (P // QUADRANT)
-        for g in range(PASSES):
-            nc.sync.dma_start(
-                scale_table[rows_of_pass * g : rows_of_pass * (g + 1), :].bitcast(I32),
-                x_scales[g].rearrange("(q r) n -> r q n", r=SCALE_ROWS).bitcast(I32),
-            )
+        nc.sync.dma_start(
+            scale_table[:QUADRANT, :].bitcast(I32),
+            x_scales.rearrange("g m n -> m g n").bitcast(I32),
+        )
         places = [load_list(pos1, "pos1"), load_list(pos2, "pos2"), load_list(pos3, "pos3"), load_list(cen, "cen")]
         x_table = [load_words(0, 15)]
         load_weight(e0, 0)
@@ -269,14 +322,14 @@ def tile_picked_edgecv_gelu_p_kernel(
         nc.vector.memset(zero[:], 0.0)
         no_bias = sb.tile([P, 1], F32, name="no_bias")
         nc.scalar.activation(no_bias[:], zero[:], GELU)
-        x_scale = new_tile([P, S], U8, "x_scale")
+        x_scale = new_tile([P, PASSES * S], U8, "x_scale")
         nc.gpsimd.memset(x_scale[:].bitcast(I32), 0)
         picked_scale = new_tile([P, S], U8, "picked_scale")
         nc.vector.tensor_copy(picked_scale[:], scale_table[:].indirect(picked[:]))
         for q in range(P // QUADRANT):
             nc.scalar.dma_start(
-                x_scale[QUADRANT * q : QUADRANT * q + SCALE_ROWS * PASSES, :].bitcast(I32),
-                picked_scale[q : QUADRANT : P // QUADRANT, :].bitcast(I32),
+                x_scale[QUADRANT * q : QUADRANT * q + SCALE_ROWS, :].bitcast(I32).rearrange("r (g n) -> r g n", g=PASSES),
+                picked_scale[SCALE_ROWS * PASSES * q : SCALE_ROWS * PASSES * (q + 1), :].bitcast(I32),
             )
         load_weight(y0, 0, 5)
         load_weight(y0, 1, 3)
@@ -346,7 +399,7 @@ def tile_picked_edgecv_gelu_p_kernel(
         gelu(0, 0)
         gelu(0, 1)
         turn(0, 2, 0, 2)
-        quantize_product(y3)
+        quantize_product(y3, 44)
         round_product(e3, 40)
         empty_both(y2)
         gelu(0, 2)
@@ -356,46 +409,44 @@ def tile_picked_edgecv_gelu_p_kernel(
         look_up(2, 1, "vector", 8)
         look_up(2, CENTRE, "scalar")
         turn(1, 1, 0, 1)
-        empty_both(y3)
+        empty_both(y3, 46)
         quantize_product(e3)
-        turn(2, 0, 6, 0)
         product(e3, 3)
-        gelu(1, 0)
+        gelu(1, 0, at=44)
         gelu(1, 1)
         turn(1, 2, 5, 2)
-        look_up(2, 2, "vector", 0)
+        look_up_sum(2, 2, 0)
         look_up(3, CENTRE, "vector", 2)
-        larger_of_two(0, 2)
-        turn(2, 1, 0, 1)
         empty_both(e3)
-        turn(2, 2, 3, 2)
+        larger_of_two(0, at=46)
+        turn(2, 0, 0, 0)
+        turn(2, 1, 3, 1)
         gelu(1, 2)
+        turn(2, 2, 4, None)
         gelu(2, 0)
         gelu(2, 1)
         gelu(2, 2)
-        look_up(3, 0, "vector", None, 0, 2)
-        features(3, 0, 4, CENTRE, 0, 2)
-        look_up(3, 1, "vector", None, 0, 2)
-        features(3, 1, 5, CENTRE, 0, 2)
-        look_up(3, 2, "vector", None, 0, 2)
-        features(3, 2, 6, CENTRE, 0, 2)
-        look_up(3, 0, "vector", None, 2, 4)
-        features(3, 0, 0, CENTRE, 2, 4)
-        look_up(3, 1, "vector", None, 2, 4)
-        features(3, 1, 3, CENTRE, 2, 4)
-        look_up(3, 2, "vector", None, 2, 4)
-        features(3, 2, 4, CENTRE, 2, 4)
-        larger_of_two(2, 4, 0, 2)
-        largest(0, 1)
-        largest(1, 2)
-        larger_of_two(2, 4, 2, 4)
-        turn_back(0, 1)
-        turn_back(1, 2)
-        largest(2, 3)
-        largest(3, 4)
-        project(0, 5)
-        project(1, 6)
-        turn_back(2, 7)
-        turn_back(3, 0)
-        project(2, 3)
-        project(3, 4)
+        look_up_sum(3, 0, None, 0, 2)
+        features(3, 0, 6, None, 0, 2)
+        look_up_sum(3, 1, None, 0, 2)
+        features(3, 1, 1, None, 0, 2)
+        look_up_sum(3, 0, None, 2, 4)
+        features(3, 0, 2, None, 2, 4)
+        look_up_sum(3, 2, None, 0, 2)
+        features(3, 2, 5, None, 0, 2)
+        look_up_sum(3, 1, None, 2, 4)
+        features(3, 1, 7, None, 2, 4)
+        larger_of_two(1)
+        look_up_sum(3, 2, None, 2, 3)
+        features(3, 2, 0, None, 2, 3)
+        look_up_sum(3, 2, None, 3, 4)
+        features(3, 2, 3, None, 3, 4)
+        larger_of_two(2)
+        larger_of_two(3, 0, 2)
+        larger_of_two(3, 2, 4)
+        for b in range(BLOCKS):
+            largest(b)
+        for b in range(BLOCKS):
+            turn_back(b, (4, 6, 1, 2)[b])
+        for b in range(BLOCKS):
+            project(b, (5, 7, 0, 3)[b])

@@ -161,10 +161,10 @@ def tile_picked_edgecv_gelu_p_kernel(
                         stop=(g == PASSES - 1 and c1 == hi),
                     )
 
-        def product(prod, number):
-            for h in range(S // BANK):
+        def product(prod, *numbers):
+            for h, number in enumerate(numbers):
                 for g in range(PASSES):
-                    multiply(prod, g, h * BANK, (h + 1) * BANK, number + h)
+                    multiply(prod, g, h * BANK, (h + 1) * BANK, number)
 
         def empty(prod, lo, hi, engine="scalar", at=None):
             name, t = prod
@@ -190,7 +190,7 @@ def tile_picked_edgecv_gelu_p_kernel(
             dst = new_tile([P, (b1 - b0) * P], F32, f"fetched{t}{d}{b0}", at)
             for b in range(b0, b1):
                 fetched[t, d, b] = dst[:, (b - b0) * P : (b - b0 + 1) * P]
-            if d == CENTRE:
+            if d == CENTRE and b1 - b0 == BLOCKS:
                 centres[t] = dst
             source = rows["y" if d == CENTRE else "e", t]
             looked_up = source[:].indirect(entries(places[d], b0 * P, b1 * P))
@@ -344,10 +344,10 @@ def tile_picked_edgecv_gelu_p_kernel(
         pick_words(1, *SPANS[0])
         round_weight(e0, 1, "scalar")
         pick_words(1, *SPANS[1])
-        quantize_weight(e0, 1, 36)
+        quantize_weight(e0, 1, 71)
         pick_words(1, *SPANS[2], 42)
-        load_product(e2, 26)
-        load_product(y2, 31)
+        load_product(e2, 31)
+        load_product(y2, 26)
         for n, (lo, hi) in enumerate(SPANS):
             multiply(e0, 1, lo, hi, n)
         round_half(y0, 0, 19)
@@ -364,89 +364,89 @@ def tile_picked_edgecv_gelu_p_kernel(
                 w3_scales[0, SCALE_ROWS * q : SCALE_ROWS * (q + 1), :].bitcast(I32),
             )
         quantize_product(y0)
-        empty(e0, *SPANS[0], "vector")
+        empty(e0, *SPANS[0], "vector", 56)
         empty(e0, *SPANS[1])
         empty(e0, *SPANS[2])
-        product(y0, 3)
+        product(y0, 3, 4)
         round_product(e1, 19)
-        round_half(y1, 0, 36)
+        round_half(y1, 0, 71)
         round_half(y1, 1)
         look_up(0, 0, "vector")
         quantize_product(e1, 17)
-        quantize_product(y1)
-        round_product(e2, 37)
-        product(e1, 0)
-        product(y1, 5)
+        quantize_product(y1, 80)
+        round_product(e2, 72)
+        product(e1, 0, 1)
+        product(y1, 5, 6)
         empty_both(y0, 22)
         look_up(0, 1, "vector", 20)
-        look_up(0, 2, "vector", 35)
-        empty_both(e1)
-        look_up(0, CENTRE, "scalar", 17)
+        look_up(0, 2, "vector", 70)
+        empty_both(e1, 64)
+        empty_both(y1, 60)
+        look_up(0, CENTRE, "scalar", 80)
         quantize_product(e2)
-        round_product(y2, 38)
-        product(e2, 0)
-        look_up(1, 0, "vector", 26)
-        look_up(1, 1, "vector", 28)
-        empty_both(y1)
-        turn(0, 0, 5, 0)
-        turn(0, 1, 6, 1)
-        empty_both(e2)
-        quantize_product(y2)
-        round_product(y3, 39)
-        product(y2, 3)
+        round_product(y2, 56)
+        product(e2, 0, 1)
         look_up(1, 2, "vector", 31)
         look_up(1, CENTRE, "vector", 33)
+        turn(0, 0, 5, 0)
+        turn(0, 1, 6, 1)
+        turn(0, 2, 3, 2)
+        empty_both(e2)
+        quantize_product(y2, 23)
+        round_product(y3, 60)
+        product(y2, 4, 7)
+        look_up(1, 0, "vector", 25)
+        look_up(1, 1, "vector", 56)
         gelu(0, 0)
         gelu(0, 1)
-        turn(0, 2, 0, 2)
-        quantize_product(y3, 44)
-        round_product(e3, 40)
-        empty_both(y2)
         gelu(0, 2)
-        turn(1, 0, 5, 0)
-        product(y3, 1)
+        turn(1, 2, 5, 2)
+        quantize_product(y3, 44)
+        round_product(e3, 64)
+        empty_both(y2)
+        product(y3, 0, 1)
+        gelu(1, 2)
+        turn(1, 0, 6, 0)
+        turn(1, 1, 3, 1)
         look_up(2, 0, "vector", 6)
         look_up(2, 1, "vector", 8)
         look_up(2, CENTRE, "scalar")
-        turn(1, 1, 0, 1)
         empty_both(y3, 46)
-        quantize_product(e3)
-        product(e3, 3)
+        quantize_product(e3, 45)
+        product(e3, 4, 7)
         gelu(1, 0, at=44)
-        gelu(1, 1)
-        turn(1, 2, 5, 2)
+        turn(2, 0, 6, 0)
         look_up_sum(2, 2, 0)
         look_up(3, CENTRE, "vector", 2)
         empty_both(e3)
         larger_of_two(0, at=46)
-        turn(2, 0, 0, 0)
+        gelu(1, 1, at=45)
+        turn(2, 2, 5, None)
         turn(2, 1, 3, 1)
-        gelu(1, 2)
-        turn(2, 2, 4, None)
         gelu(2, 0)
-        gelu(2, 1)
+        look_up(3, 0, "scalar", None, 2, 4)
         gelu(2, 2)
+        gelu(2, 1)
         look_up_sum(3, 0, None, 0, 2)
-        features(3, 0, 6, None, 0, 2)
+        features(3, 0, 0, None, 0, 2)
         look_up_sum(3, 1, None, 0, 2)
         features(3, 1, 1, None, 0, 2)
-        look_up_sum(3, 0, None, 2, 4)
-        features(3, 0, 2, None, 2, 4)
+        features(3, 0, 2, CENTRE, 2, 4)
         look_up_sum(3, 2, None, 0, 2)
-        features(3, 2, 5, None, 0, 2)
+        features(3, 2, 4, None, 0, 2)
         look_up_sum(3, 1, None, 2, 4)
         features(3, 1, 7, None, 2, 4)
-        larger_of_two(1)
         look_up_sum(3, 2, None, 2, 3)
-        features(3, 2, 0, None, 2, 3)
+        features(3, 2, 6, None, 2, 3)
         look_up_sum(3, 2, None, 3, 4)
         features(3, 2, 3, None, 3, 4)
+        larger_of_two(1)
         larger_of_two(2)
         larger_of_two(3, 0, 2)
         larger_of_two(3, 2, 4)
         for b in range(BLOCKS):
             largest(b)
         for b in range(BLOCKS):
-            turn_back(b, (4, 6, 1, 2)[b])
+            turn_back(b, (5, 0, 1, 2)[b])
         for b in range(BLOCKS):
-            project(b, (5, 7, 0, 3)[b])
+            project(b, (4, 7, 6, 3)[b])

from contextlib import ExitStack

import concourse.mybir as mybir
from concourse.masks import make_identity

K, T, S, V, H, N = 1024, 2048, 1024, 512, 512, 128
FLOPS = 2 * (2 * K * H * S + H * N * V)

F32 = mybir.dt.float32
BF16 = mybir.dt.bfloat16
I32 = mybir.dt.int32
U32 = mybir.dt.uint32
U16 = mybir.dt.uint16
U8 = mybir.dt.uint8
E4M3 = mybir.dt.float8_e4m3fn_x4
E2M1 = mybir.dt.float4_e2m1fn_x4
GELU = mybir.ActivationFunctionType.Gelu_apprx_tanh
COPY = mybir.ActivationFunctionType.Copy
MAX = mybir.AluOpType.max
MULT = mybir.AluOpType.mult
ADD = mybir.AluOpType.add

P = 128
PACK = 4
PASSES = K // (P * PACK)
BANK = 512
QUADRANT = 32
SCALE_ROWS = 4
PER_COLUMN = 16
TILES = H // P
LAST = TILES - 1
BLOCKS = V // P
EDGES = 3
CENTRE = EDGES
SPANS = ((0, BANK), (BANK, BANK + BANK // 2), (BANK + BANK // 2, S))
KB = 1024


def tile_picked_edgecv_gelu_p_kernel(
    tc, x_words, x_scales, w1, w2, w3_words, w3_scales, offs, cen, pos1, pos2, pos3, out
):
    nc = tc.nc
    with ExitStack() as ctx:
        lists = ctx.enter_context(tc.tile_pool(name="lists", bufs=1))
        sb = ctx.enter_context(tc.tile_pool(name="sb", bufs=1))
        shared = ctx.enter_context(tc.tile_pool(name="shared", bufs=1))
        psum = ctx.enter_context(tc.psum_pool(name="psum", bufs=1))

        def new_tile(shape, dtype, name, at=None):
            if at is None:
                return sb.tile(shape, dtype, name=name, align_bytes=64)
            return shared.tile(shape, dtype, name=name, align_bytes=64, offset=int(at * KB))

        def bank(number):
            return f"bank{number}"

        weights = {"e": w2, "y": w1}

        def load_list(src, name):
            dst = lists.tile(list(src.shape), U16, name=name)
            nc.sync.dma_start(dst[:], src)
            return dst

        def load_words(g, at=None):
            dst = new_tile([P, T], U32, f"x_table{g}", at)
            nc.sync.dma_start(dst[:].bitcast(I32), x_words[g].rearrange("p n j -> p (n j)").bitcast(I32))
            return dst

        raw, w_code, w_scale, w_bf, rows, fetched = {}, {}, {}, {}, {}, {}

        def load_weight(prod, g, at=None):
            name, t = prod
            raw[prod, g] = new_tile([P, PACK, P], F32, f"raw_{name}{t}_{g}", at)
            src = weights[name][g * P * PACK : (g + 1) * P * PACK, t * P : (t + 1) * P]
            nc.sync.dma_start(raw[prod, g][:], src.rearrange("(p j) c -> p j c", j=PACK))

        def entries(index, lo, hi):
            return index[:, lo // PER_COLUMN : hi // PER_COLUMN]

        x_code = [[] for g in range(PASSES)]

        def pick_words(g, lo, hi, at=None):
            dst = new_tile([P, hi - lo], U32, f"x_code{g}_{lo}", at)
            nc.vector.tensor_copy(dst[:], x_table[g][:].indirect(entries(picked, lo, hi)))
            x_code[g].append((lo, hi, dst))

        def round_weight(prod, g, engine, at=None):
            name, t = prod
            w_bf[prod, g] = new_tile([P, P, PACK], BF16, f"w_bf_{name}{t}_{g}", at)
            if engine == "scalar":
                nc.scalar.copy(
                    w_bf[prod, g][:].rearrange("p (c i) j -> p c j i", i=PACK),
                    raw[prod, g][:].rearrange("p j (c i) -> p c j i", i=PACK),
                )
            elif engine == "vector":
                nc.vector.tensor_copy(w_bf[prod, g][:], raw[prod, g][:].rearrange("p j c -> p c j"))
            else:
                nc.gpsimd.tensor_scalar(w_bf[prod, g][:], raw[prod, g][:].rearrange("p j c -> p c j"), 1.0, 0.0, MULT, ADD)

        def round_product(prod, at):
            name, t = prod
            both = new_tile([P, PASSES, P, PACK], BF16, f"w_bf_{name}{t}", at)
            w_bf[prod] = both
            nc.gpsimd.tensor_scalar(both[:], raw[prod][:].rearrange("p g j c -> p g c j"), 1.0, 0.0, MULT, ADD)

        def round_half(prod, g, at=None):
            name, t = prod
            if g == 0:
                w_bf[prod] = new_tile([P, PASSES, P, PACK], BF16, f"w_bf_{name}{t}", at)
            nc.scalar.copy(
                w_bf[prod][:, g].rearrange("p (c i) j -> p c j i", i=PACK),
                raw[prod, g][:].rearrange("p j (c i) -> p c j i", i=PACK),
            )

        def load_product(prod, at=None):
            name, t = prod
            raw[prod] = new_tile([P, PASSES, PACK, P], F32, f"raw_{name}{t}", at)
            for g in range(PASSES):
                src = weights[name][g * P * PACK : (g + 1) * P * PACK, t * P : (t + 1) * P]
                nc.sync.dma_start(raw[prod][:, g], src.rearrange("(p j) c -> p j c", j=PACK))

        def quantize_product(prod, at=None):
            name, t = prod
            code = new_tile([P, PASSES, P], U32, f"w_code_{name}{t}", at)
            scale = new_tile([P, PASSES, P], U8, f"w_scale_{name}{t}")
            for g in range(PASSES):
                w_code[prod, g], w_scale[prod, g] = code[:, g], scale[:, g]
            nc.vector.quantize_mx(
                out=code[:].rearrange("p g c -> p (g c)").bitcast(E4M3),
                scales=scale[:].rearrange("p g c -> p (g c)"),
                in_=w_bf[prod][:].rearrange("p g c j -> p (g c j)"),
            )

        def quantize_weight(prod, g, at=None):
            name, t = prod
            w_code[prod, g] = new_tile([P, P], U32, f"w_code_{name}{t}_{g}", at)[:]
            w_scale[prod, g] = new_tile([P, P], U8, f"w_scale_{name}{t}_{g}")[:]
            nc.vector.quantize_mx(
                out=w_code[prod, g].bitcast(E4M3),
                scales=w_scale[prod, g],
                in_=w_bf[prod, g][:].rearrange("p c j -> p (c j)"),
            )

        accs = {}

        def multiply(prod, g, lo, hi, number):
            name, t = prod
            if g == 0:
                accs[prod, lo] = psum.tile([P, hi - lo], F32, name=f"acc_{name}{t}_{lo}", tag=bank(number))
            acc = accs[prod, lo]
            for first, end, words in x_code[g]:
                c0, c1 = max(lo, first), min(hi, end)
                if c0 < c1:
                    nc.tensor.matmul_mx(
                        out=acc[:, c0 - lo : c1 - lo],
                        lhsT=w_code[prod, g].bitcast(E4M3),
                        lhsT_scale=w_scale[prod, g],
                        rhs=words[:, c0 - first : c1 - first].bitcast(E4M3),
                        rhs_scale=x_scale[:, g * S + c0 : g * S + c1],
                        start=(g == 0),
                        stop=(g == PASSES - 1 and c1 == hi),
                    )

        def product(prod, *numbers):
            for h, number in enumerate(numbers):
                for g in range(PASSES):
                    multiply(prod, g, h * BANK, (h + 1) * BANK, number)

        def empty(prod, lo, hi, engine="scalar", at=None):
            name, t = prod
            if prod not in rows:
                rows[prod] = new_tile([P, S], F32, f"rows_{name}{t}", at)
            copy = nc.scalar.copy if engine == "scalar" else nc.vector.tensor_copy
            copy(rows[prod][:, lo:hi], accs[prod, lo][:])

        def empty_both(prod, at=None):
            for h in range(S // BANK):
                empty(prod, h * BANK, (h + 1) * BANK, "scalar", at)

        def look_up_sum(t, d, at=None, b0=0, b1=BLOCKS):
            dst = new_tile([P, (b1 - b0) * P], F32, f"summed{t}{d}{b0}", at)
            for b in range(b0, b1):
                fetched[t, d, b] = dst[:, (b - b0) * P : (b - b0 + 1) * P]
            looked_up = rows["e", t][:].indirect(entries(places[d], b0 * P, b1 * P))
            nc.vector.tensor_tensor(dst[:], looked_up, centres[t][:, b0 * P : b1 * P], ADD)

        centres = {}

        def look_up(t, d, engine="vector", at=None, b0=0, b1=BLOCKS):
            dst = new_tile([P, (b1 - b0) * P], F32, f"fetched{t}{d}{b0}", at)
            for b in range(b0, b1):
                fetched[t, d, b] = dst[:, (b - b0) * P : (b - b0 + 1) * P]
            if d == CENTRE and b1 - b0 == BLOCKS:
                centres[t] = dst
            source = rows["y" if d == CENTRE else "e", t]
            looked_up = source[:].indirect(entries(places[d], b0 * P, b1 * P))
            if engine == "scalar":
                nc.scalar.activation(dst[:], looked_up, COPY)
            else:
                nc.vector.tensor_copy(dst[:], looked_up)

        feats = {}
        third = sb.tile([P, BLOCKS, 2, TILES, P // 2], BF16, name="third")
        pairs = []
        z_row = sb.tile([P, BLOCKS, 2, TILES, P // 2], BF16, name="z_row")
        sums = {}

        def turn(t, d, number, opens, b0=0, b1=BLOCKS):
            sums[t, d, b0] = psum.tile([P, b1 - b0, P], F32, name=f"sums{t}{d}{b0}", tag=bank(number))
            if opens is None:
                for b in range(b0, b1):
                    nc.tensor.transpose(sums[t, d, b0][:, b - b0], fetched[t, d, b], identity[:])
                return
            adds = d if opens == CENTRE else CENTRE
            for b in range(b0, b1):
                nc.tensor.matmul(sums[t, d, b0][:, b - b0], fetched[t, opens, b], identity[:], start=(b == b0), stop=False, is_transpose=True)
            for b in range(b0, b1):
                nc.tensor.matmul(sums[t, d, b0][:, b - b0], fetched[t, adds, b], identity[:], start=False, stop=(b == b1 - 1), is_transpose=True)

        def gelu(t, d, b0=0, b1=BLOCKS, at=None):
            if d == EDGES - 1:
                dst = third[:, b0:b1, :, t].rearrange("p b u (m o) -> p u b m o", o=2)
            else:
                if (t, d) not in feats:
                    feats[t, d] = new_tile([P, 2, BLOCKS, P // 2], BF16, f"feats{t}{d}", at)
                dst = feats[t, d][:, :, b0:b1].rearrange("p u b (m o) -> p u b m o", o=2)
            nc.scalar.activation(
                dst,
                sums[t, d, b0][:].rearrange("p b (m u o) -> p u b m o", u=2, o=2),
                GELU,
                bias=no_bias[:],
            )

        def features(t, d, number, opens, b0=0, b1=BLOCKS):
            turn(t, d, number, opens, b0, b1)
            gelu(t, d, b0, b1)

        def larger_of_two(t, b0=0, b1=BLOCKS, at=None):
            if not pairs:
                pairs.append(new_tile([P, BLOCKS, 2, TILES, P // 2], BF16, "pair", at))
            dst = pairs[0][:, b0:b1, :, t].rearrange("p b u c -> p u b c")
            nc.vector.tensor_tensor(dst, feats[t, 0][:, :, b0:b1], feats[t, 1][:, :, b0:b1], MAX)

        def largest(b):
            nc.vector.tensor_tensor(z_row[:, b], pairs[0][:, b], third[:, b], MAX)

        def turn_words(src, b, number, name):
            words = src[:, b].rearrange("p u t c -> p (u t c)").bitcast(F32)
            turned = psum.tile([P, 2, P], F32, name=f"{name}{b}", tag=bank(number))
            for u in range(2):
                nc.tensor.transpose(turned[:, u], words[:, u * P : (u + 1) * P], identity[:])
            return turned

        pair_turned = {}

        def turn_pair(b, number, engine="scalar"):
            turned = turn_words(pairs[0], b, number, "pair_words")
            pair_turned[b] = new_tile([P, P, PACK], BF16, f"pair_turned{b}")
            copy = nc.scalar.copy if engine == "scalar" else nc.vector.tensor_copy
            copy(pair_turned[b][:].bitcast(F32), turned[:].rearrange("p u v -> p v u"))

        def largest_turned(b, number):
            turned = turn_words(third, b, number, "third_words")
            z_bf[b] = new_tile([P, P, PACK], BF16, f"z_bf{b}")
            nc.vector.tensor_tensor(
                z_bf[b][:].rearrange("p v (u o) -> p v u o", o=2),
                turned[:].bitcast(BF16).rearrange("p u (v o) -> p v u o", o=2),
                pair_turned[b][:].rearrange("p v (u o) -> p v u o", o=2),
                MAX,
            )

        z_bf, z_code, z_scale, result = {}, {}, {}, {}

        def turn_back(b, number, engine="scalar"):
            words = z_row[:, b].rearrange("p u t c -> p (u t c)").bitcast(F32)
            turned = psum.tile([P, 2, P], F32, name=f"turned{b}", tag=bank(number))
            for u in range(2):
                nc.tensor.transpose(turned[:, u], words[:, u * P : (u + 1) * P], identity[:])
            z_bf[b] = new_tile([P, P, PACK], BF16, f"z_bf{b}")
            copy = nc.scalar.copy if engine == "scalar" else nc.vector.tensor_copy
            copy(z_bf[b][:].bitcast(F32), turned[:].rearrange("p u v -> p v u"))

        def project(b, number, engine="scalar"):
            z_code[b] = new_tile([P, P], U32, f"z_code{b}")
            z_scale[b] = new_tile([P, P], U8, f"z_scale{b}")
            nc.vector.quantize_mx(out=z_code[b][:].bitcast(E4M3), scales=z_scale[b][:], in_=z_bf[b][:].rearrange("p v j -> p (v j)"))
            acc = psum.tile([P, P], F32, name=f"out{b}", tag=bank(number))
            nc.tensor.matmul_mx(
                out=acc[:],
                lhsT=w3_code[:].bitcast(E2M1),
                lhsT_scale=w3_scale[:],
                rhs=z_code[b][:].bitcast(E4M3),
                rhs_scale=z_scale[b][:],
                start=True,
                stop=True,
            )
            result[b] = new_tile([P, P], F32, f"result{b}")
            copy = nc.scalar.copy if engine == "scalar" else nc.vector.tensor_copy
            copy(result[b][:], acc[:])
            nc.sync.dma_start(out[:, b * P : (b + 1) * P], result[b][:])

        e0, e1, e2, e3 = (("e", t) for t in range(TILES))
        y0, y1, y2, y3 = (("y", t) for t in range(TILES))


        scale_table = new_tile([P, T], U8, "scale_table", 4)
        nc.vector.memset(scale_table[QUADRANT : 2 * QUADRANT, :].bitcast(I32), 0)
        nc.vector.memset(scale_table[2 * QUADRANT :, :].bitcast(I32), 0)
        picked = load_list(offs, "offs")
        nc.sync.dma_start(
            scale_table[:QUADRANT, :].bitcast(I32),
            x_scales.rearrange("g m n -> m g n").bitcast(I32),
        )
        places = [load_list(pos1, "pos1"), load_list(pos2, "pos2"), load_list(pos3, "pos3"), load_list(cen, "cen")]
        x_table = [load_words(0, 15)]
        load_weight(e0, 0)
        x_table.append(load_words(1, 26))
        load_weight(e0, 1, 42)
        identity = sb.tile([P, P], F32, name="identity")
        make_identity(nc, identity[:])
        zero = sb.tile([P, 1], F32, name="zero")
        nc.vector.memset(zero[:], 0.0)
        no_bias = sb.tile([P, 1], F32, name="no_bias")
        nc.scalar.activation(no_bias[:], zero[:], GELU)
        x_scale = new_tile([P, PASSES * S], U8, "x_scale")
        nc.gpsimd.memset(x_scale[:].bitcast(I32), 0)
        picked_scale = new_tile([P, S], U8, "picked_scale")
        nc.vector.tensor_copy(picked_scale[:], scale_table[:].indirect(picked[:]))
        for q in range(P // QUADRANT):
            nc.scalar.dma_start(
                x_scale[QUADRANT * q : QUADRANT * q + SCALE_ROWS, :].bitcast(I32).rearrange("r (g n) -> r g n", g=PASSES),
                picked_scale[SCALE_ROWS * PASSES * q : SCALE_ROWS * PASSES * (q + 1), :].bitcast(I32),
            )
        load_weight(y0, 0, 5)
        load_weight(y0, 1, 3)
        pick_words(0, 0, S)
        load_product(e1, 12)
        load_weight(y1, 0, 16)
        load_weight(y1, 1, 21)
        round_weight(e0, 0, "scalar")
        quantize_weight(e0, 0)
        for n, (lo, hi) in enumerate(SPANS):
            multiply(e0, 0, lo, hi, n)
        pick_words(1, *SPANS[0])
        round_weight(e0, 1, "scalar")
        pick_words(1, *SPANS[1])
        quantize_weight(e0, 1, 71)
        pick_words(1, *SPANS[2], 42)
        load_product(e2, 31)
        load_product(y2, 26)
        for n, (lo, hi) in enumerate(SPANS):
            multiply(e0, 1, lo, hi, n)
        round_half(y0, 0, 19)
        round_half(y0, 1)
        load_product(y3, 6)
        load_product(e3, 0)
        w3_code = new_tile([P, 2 * N], U8, "w3_code", 30)
        nc.sync.dma_start(w3_code[:].bitcast(I32), w3_words[0].bitcast(I32))
        w3_scale = new_tile([P, N], U8, "w3_scale", 30.5)
        nc.vector.memset(w3_scale[:].bitcast(I32), 0)
        for q in range(P // QUADRANT):
            nc.sync.dma_start(
                w3_scale[QUADRANT * q : QUADRANT * q + SCALE_ROWS, :].bitcast(I32),
                w3_scales[0, SCALE_ROWS * q : SCALE_ROWS * (q + 1), :].bitcast(I32),
            )
        quantize_product(y0)
        empty(e0, *SPANS[0], "vector", 56)
        empty(e0, *SPANS[1])
        empty(e0, *SPANS[2])
        product(y0, 3, 4)
        round_product(e1, 19)
        round_half(y1, 0, 71)
        round_half(y1, 1)
        look_up(0, 0, "vector")
        quantize_product(e1, 17)
        quantize_product(y1, 80)
        round_product(e2, 72)
        product(e1, 0, 1)
        product(y1, 5, 6)
        empty_both(y0, 22)
        look_up(0, 1, "vector", 20)
        look_up(0, 2, "vector", 70)
        empty_both(e1, 64)
        empty_both(y1, 60)
        look_up(0, CENTRE, "scalar", 80)
        quantize_product(e2)
        round_product(y2, 56)
        product(e2, 0, 1)
        look_up(1, 2, "vector", 31)
        look_up(1, CENTRE, "vector", 33)
        turn(0, 0, 5, 0)
        turn(0, 1, 6, 1)
        turn(0, 2, 3, 2)
        empty_both(e2)
        quantize_product(y2, 23)
        round_product(y3, 60)
        product(y2, 4, 7)
        look_up(1, 0, "vector", 25)
        look_up(1, 1, "vector", 56)
        gelu(0, 0)
        gelu(0, 1)
        gelu(0, 2)
        turn(1, 2, 5, 2)
        quantize_product(y3, 44)
        round_product(e3, 64)
        empty_both(y2)
        product(y3, 0, 1)
        gelu(1, 2)
        turn(1, 0, 6, 0)
        turn(1, 1, 3, 1)
        look_up(2, 0, "vector", 6)
        look_up(2, 1, "vector", 8)
        look_up(2, CENTRE, "scalar")
        empty_both(y3, 46)
        quantize_product(e3, 45)
        product(e3, 4, 7)
        gelu(1, 0, at=44)
        turn(2, 0, 6, 0)
        look_up_sum(2, 2, 0)
        look_up(3, CENTRE, "vector", 2)
        empty_both(e3)
        larger_of_two(0, at=46)
        gelu(1, 1, at=45)
        turn(2, 2, 5, None)
        turn(2, 1, 3, 1)
        gelu(2, 0)
        look_up(3, 0, "scalar", None, 2, 4)
        gelu(2, 2)
        gelu(2, 1)
        look_up_sum(3, 0, None, 0, 2)
        features(3, 0, 0, None, 0, 2)
        look_up_sum(3, 1, None, 0, 2)
        features(3, 1, 1, None, 0, 2)
        features(3, 0, 2, CENTRE, 2, 4)
        look_up_sum(3, 2, None, 0, 2)
        features(3, 2, 4, None, 0, 2)
        look_up_sum(3, 1, None, 2, 4)
        features(3, 1, 7, None, 2, 4)
        look_up_sum(3, 2, None, 2, 3)
        features(3, 2, 6, None, 2, 3)
        look_up_sum(3, 2, None, 3, 4)
        features(3, 2, 3, None, 3, 4)
        larger_of_two(1)
        larger_of_two(2)
        larger_of_two(3, 0, 2)
        larger_of_two(3, 2, 4)
        for b in range(BLOCKS):
            largest(b)
        for b in range(BLOCKS):
            turn_back(b, (5, 0, 1, 2)[b])
        for b in range(BLOCKS):
            project(b, (4, 7, 6, 3)[b])
